import numpy as np
import ml_dtypes


def mxq(x, axis, fmt="e4m3"):
    dtype, down = {"e4m3": (ml_dtypes.float8_e4m3fn, 7), "e5m2": (ml_dtypes.float8_e5m2, 14)}[fmt]
    v = np.moveaxis(np.asarray(x, np.float32).astype(ml_dtypes.bfloat16).astype(np.float64), axis, -1)
    blocks = v.reshape(v.shape[:-1] + (-1, 32))
    amax = np.abs(blocks).max(-1, keepdims=True)
    byte = np.maximum(np.where(amax > 0, np.frexp(amax)[1] - 1 + 127, 0) - down, 1)
    scale = np.exp2(byte - 127.0)
    codes = (blocks / scale).astype(np.float32).astype(dtype).astype(np.float64)
    return np.moveaxis((codes * scale).reshape(v.shape), -1, axis)


WIDE = False


def mx_kscale(k):
    if not WIDE:
        return np.ones(k)
    levels = np.array([10, -10, 5, -5, 0])
    if k % 512:
        return np.exp2(np.random.permutation(np.resize(levels, k // 32))).repeat(32)
    a = np.empty((k // 512, 16))
    for p in range(k // 512):
        a[p, :8] = np.random.permutation(np.resize(levels, 8))
        for g in range(8):
            far = levels[np.abs(levels - a[p, g]) >= 10]
            a[p, g + 8] = far[np.random.randint(len(far))]
    return np.exp2(a.ravel()).repeat(32)


def f64(x):
    return np.asarray(x).astype(np.float64)


def striped(idx):
    return np.tile(idx.reshape(-1, 16).T, (8, 1)).astype(np.uint16)


def unstriped(offs):
    return offs[:16].T.reshape(-1).astype(np.int64)


def pack_weight(w):
    k, n = w.shape
    w = f64(np.asarray(w, np.float32).astype(ml_dtypes.bfloat16)).reshape(k // 32, 32, n)
    amax = np.abs(w).max(1)
    byte = np.clip(np.where(amax > 0, np.frexp(amax)[1] - 1 + 127 - 7, 1), 1, 254)
    scaled = (w * np.exp2(127.0 - byte)[:, None, :]).reshape(k, n).astype(np.float32)
    words = np.ascontiguousarray(scaled.reshape(k // 512, 128, 4, n).transpose(0, 1, 3, 2)).astype(ml_dtypes.float8_e4m3fn).view(np.uint8)
    return words, np.ascontiguousarray(byte.astype(np.uint8).reshape(k // 512, 16, n))


def unpack_weight(words, scales):
    g, p, n, _ = words.shape
    vals = np.ascontiguousarray(words).view(ml_dtypes.float8_e4m3fn).astype(np.float64) * np.repeat(np.exp2(scales.astype(np.float64) - 127.0), 8, axis=1)[..., None]
    return vals.transpose(0, 1, 3, 2).reshape(g * 512, n)


K, T, S, H, D, W, U = 1024, 1024, 512, 512, 8, 2048, 1024
P = 2 ** 7


def setup_inputs():
    n = np.random.standard_normal
    s = mx_kscale(K)[:, None]
    u = mx_kscale(H)
    packed_xT = pack_weight(n((K, T)) * s)
    packed_eT = pack_weight(n((H, W)) / np.sqrt(H) / u[:, None])
    return {
        "x_words": packed_xT[0],
        "x_scales": packed_xT[1],
        "w1": (n((K, H)) / np.sqrt(K) / s * u).astype(np.float32),
        "e_words": packed_eT[0],
        "e_scales": packed_eT[1],
        "half": (np.tile(np.random.uniform(0.2, 1.0, W), (P, 1))).astype(np.float32),
        "val": (np.tile(n(W), (P, 1))).astype(np.float32),
        "offs": striped(np.random.permutation(T)[:S]),
        "ex": striped(np.random.permutation(W)[:U]),
    }


def reference(x_words, x_scales, w1, e_words, e_scales, half, val, offs, ex):
    xq = unpack_weight(x_words, x_scales)[:, unstriped(offs)]
    h = mxq(f64(w1), 0, "e4m3").T @ xq
    e_ex = unpack_weight(e_words, e_scales)[:, unstriped(ex)]
    y = mxq(h, 0, "e4m3").T @ e_ex
    ee = np.exp(0.5 * y - (f64(half)[:1][:, unstriped(ex)]))
    gg = ee * (f64(val)[:1][:, unstriped(ex)])
    num = gg.reshape(len(gg), -1, D).sum(axis=2)
    den = ee.reshape(len(ee), -1, D).sum(axis=2)
    return num / den

@@ -1,0 +1,190 @@
+from contextlib import ExitStack
+
+import concourse.mybir as mybir
+from concourse.masks import make_identity
+
+F32 = mybir.dt.float32
+BF16 = mybir.dt.bfloat16
+I32 = mybir.dt.int32
+U32 = mybir.dt.uint32
+U16 = mybir.dt.uint16
+U8 = mybir.dt.uint8
+FP8X4 = mybir.dt.float8_e4m3fn_x4
+MULT = mybir.AluOpType.mult
+ADD = mybir.AluOpType.add
+EXP = mybir.ActivationFunctionType.Exp
+RSQRT = mybir.ActivationFunctionType.Abs_reciprocal_sqrt
+SQUARE = mybir.ActivationFunctionType.Square
+
+P = 128
+K, T, S, H, D, W, U = 1024, 1024, 512, 512, 8, 2048, 1024
+V = U // D
+PASSES = K // 512
+FLOPS = 2 * K * H * S + 2 * H * S * U
+
+
+def tile_picked_ynw_avg_p_kernel(
+    tc, x_words, x_scales, w1, e_words, e_scales, half, val, offs, ex, out
+):
+    nc = tc.nc
+    with ExitStack() as ctx:
+        keep = ctx.enter_context(tc.tile_pool(name="keep", bufs=1))
+        shared = ctx.enter_context(tc.tile_pool(name="shared", bufs=1))
+        banks = ctx.enter_context(tc.psum_pool(name="banks", bufs=5))
+        sums = ctx.enter_context(tc.psum_pool(name="sums", bufs=1))
+
+        ex_list = keep.tile([P, U // 16], U16, name="ex_list")
+        offs_list = keep.tile([P, S // 16], U16, name="offs_list")
+        half_win = keep.tile([P, W], F32, name="half_win")
+        val_win = keep.tile([P, W], F32, name="val_win")
+        es_win = keep.tile([P, W], U8, name="es_win")
+        xs_win = keep.tile([P, T], U8, name="xs_win")
+        ew_win = keep.tile([P, W], I32, name="ew_win")
+        xw_win = [keep.tile([P, T], I32, name="xw_win%d" % o) for o in range(PASSES)]
+        w_raw = [[keep.tile([P, 4, H // 2], F32, name="w_raw%d%d" % (o, u)) for u in range(2)] for o in range(PASSES)]
+
+        zero = keep.tile([P, 1], F32, name="zero")
+        nc.vector.memset(zero[:], 0.0)
+        nc.vector.memset(xs_win[:].bitcast(I32), 0)
+        nc.vector.memset(es_win[:].bitcast(I32), 0)
+        nc.vector.memset(half_win[0 : P - 1, :], 0.0)
+        nc.scalar.copy(val_win[0 : P - 1, :], zero[0 : P - 1, :].to_broadcast([P - 1, W]))
+
+        def load_w(o, u):
+            rows = w1[o * 512 : (o + 1) * 512, u * (H // 2) : (u + 1) * (H // 2)]
+            nc.sync.dma_start(w_raw[o][u][:], rows.rearrange("(p j) c -> p j c", j=4))
+
+        nc.sync.dma_start(ex_list[:], ex)
+        nc.sync.dma_start(half_win[P - 1 : P, :], half[0:1, :])
+        nc.sync.dma_start(val_win[P - 1 : P, :], val[0:1, :])
+        nc.sync.dma_start(offs_list[:], offs)
+        for o in range(PASSES):
+            nc.sync.dma_start(xw_win[o][:], x_words[o].rearrange("p n t -> p (n t)").bitcast(I32))
+        for q in range(4):
+            nc.sync.dma_start(xs_win[32 * q : 32 * q + 8, :].bitcast(I32), x_scales[:, 4 * q : 4 * q + 4, :].bitcast(I32))
+        for o in range(PASSES):
+            for u in range(2):
+                load_w(o, u)
+        nc.sync.dma_start(ew_win[:], e_words[0].rearrange("p n t -> p (n t)").bitcast(I32))
+        for q in range(4):
+            nc.sync.dma_start(es_win[32 * q : 32 * q + 4, :].bitcast(I32), e_scales[0, 4 * q : 4 * q + 4, :].bitcast(I32))
+
+        ident = keep.tile([P, P], F32, name="ident")
+        make_identity(nc, ident[:])
+
+        half_ex = keep.tile([P, U], F32, name="half_ex")
+        val_ex = keep.tile([P, U], F32, name="val_ex")
+        nc.vector.tensor_copy(half_ex[:], half_win[:].indirect(ex_list[:]))
+        nc.vector.tensor_copy(val_ex[:], val_win[:].indirect(ex_list[:]))
+        half_col = keep.tile([P, D], F32, name="half_col")
+        val_col = keep.tile([P, D], F32, name="val_col")
+        nc.gpsimd.dma_start(half_col[:], half_ex[P - 1 : P, :].rearrange("o (v d) -> o v d", d=D))
+        nc.gpsimd.dma_start(val_col[:], val_ex[P - 1 : P, :].rearrange("o (v d) -> o v d", d=D))
+        neg_half = keep.tile([P, D], F32, name="neg_half")
+        nc.gpsimd.tensor_scalar(neg_half[:], half_col[:], -1.0, 0.0, MULT, ADD)
+
+        xw = []
+        for o in range(PASSES):
+            words = keep.tile([P, S], U32, name="xw%d" % o, align_bytes=64)
+            nc.vector.tensor_copy(words[:], xw_win[o][:].bitcast(U32).indirect(offs_list[:]))
+            xw.append(words)
+        xs = keep.tile([P, S], U8, name="xs", align_bytes=64)
+        nc.vector.tensor_copy(xs[:], xs_win[:].indirect(offs_list[:]))
+
+        w_codes = []
+        w_scales = []
+        for o in range(PASSES):
+            w_bf = keep.tile([P, 4 * H], BF16, name="w_bf%d" % o, align_bytes=64)
+            dst = w_bf[:].rearrange("p (t m j) -> p m t j", t=4, j=4)
+            for u in range(2):
+                nc.scalar.copy(dst[:, 64 * u : 64 * (u + 1), :, :], w_raw[o][u][:].rearrange("p j (m t) -> p m t j", t=4))
+            codes = keep.tile([P, H], U32, name="w_codes%d" % o, align_bytes=64)
+            scales = keep.tile([P, H], U8, name="w_scales%d" % o, align_bytes=64)
+            nc.vector.quantize_mx(codes[:].bitcast(FP8X4), scales[:], w_bf[:])
+            w_codes.append(codes)
+            w_scales.append(scales)
+
+        ew_ex = keep.tile([P, U], U32, name="ew_ex")
+        es_ex = keep.tile([P, U], U8, name="es_ex")
+        nc.vector.tensor_copy(ew_ex[:], ew_win[:].bitcast(U32).indirect(ex_list[:]))
+        nc.vector.tensor_copy(es_ex[:], es_win[:].indirect(ex_list[:]))
+
+        h_bf = shared.tile([P, S, 4], BF16, name="h_bf", align_bytes=64, offset=0)
+        h_codes = keep.tile([P, S], U32, name="h_codes", align_bytes=64)
+        h_scales = keep.tile([P, S], U8, name="h_scales", align_bytes=64)
+        for b in range(4):
+            cols = slice(P * b, P * (b + 1))
+            h_ps = banks.tile([P, 4, P], F32, name="h_ps", tag="bank")
+            for t in range(4):
+                for o in range(PASSES):
+                    nc.tensor.matmul_mx(
+                        h_ps[:, t, :],
+                        lhsT=w_codes[o][:, P * t : P * (t + 1)].bitcast(FP8X4),
+                        lhsT_scale=w_scales[o][:, P * t : P * (t + 1)],
+                        rhs=xw[o][:, cols].bitcast(FP8X4),
+                        rhs_scale=xs[4 * o : P, cols],
+                        start=(o == 0),
+                        stop=(o == PASSES - 1),
+                    )
+            nc.scalar.copy(h_bf[:, cols, :], h_ps[:].rearrange("p t n -> p n t"))
+
+        def deal(a, codes, scales):
+            nc.vector.tensor_copy(
+                codes[:].rearrange("p (b vq vl) -> p vq b vl", b=4, vl=4),
+                ew_ex[:].rearrange("p (vq vl a b) -> p a vq b vl", a=2, b=4, vl=4)[:, a],
+            )
+            nc.vector.tensor_copy(
+                scales[:].rearrange("p (b v) -> p v b", b=4),
+                es_ex[:].rearrange("p (v a b) -> p a v b", a=2, b=4)[:, a],
+            )
+
+        e_codes = [keep.tile([P, U // 2], U32, name="e_codes0", align_bytes=64)]
+        e_bytes = [keep.tile([P, U // 2], U8, name="e_bytes0", align_bytes=64)]
+        deal(0, e_codes[0], e_bytes[0])
+        nc.vector.quantize_mx(h_codes[:].bitcast(FP8X4), h_scales[:], h_bf[:].rearrange("p n t -> p (n t)"))
+        e_codes.append(shared.tile([P, U // 2], U32, name="e_codes1", align_bytes=64, offset=0))
+        e_bytes.append(shared.tile([P, U // 2], U8, name="e_bytes1", align_bytes=64, offset=2048))
+        deal(1, e_codes[1], e_bytes[1])
+
+        den = [sums.tile([P, 2, V], F32, name="den%d" % g) for g in range(2)]
+        num = sums.tile([P, 4, V], F32, name="num")
+        acc = [keep.tile([P, S], F32, name="acc%d" % i) for i in range(2)]
+        for d in range(D):
+            y_ps = banks.tile([P, S], F32, name="y_ps", tag="bank")
+            cols = slice(V * (d % 4), V * (d % 4 + 1))
+            nc.tensor.matmul_mx(
+                y_ps[:],
+                lhsT=e_codes[d // 4][:, cols].bitcast(FP8X4),
+                lhsT_scale=e_bytes[d // 4][:, cols],
+                rhs=h_codes[:].bitcast(FP8X4),
+                rhs_scale=h_scales[:],
+                start=True,
+                stop=True,
+            )
+            ee = keep.tile([P, S], F32, name="ee%d" % d)
+            nc.scalar.activation(ee[:], y_ps[:], EXP, bias=neg_half[:, d : d + 1], scale=0.5)
+            for b in range(4):
+                nc.tensor.matmul(
+                    den[b // 2][:, b % 2, :], ee[:, P * b : P * (b + 1)], ident[:],
+                    is_transpose=True, start=(d == 0 and b % 2 == 0), stop=(d == D - 1 and b % 2 == 1),
+                )
+            if d < 2:
+                nc.vector.tensor_scalar(acc[d][:], ee[:], val_col[:, d : d + 1], None, MULT)
+            else:
+                nc.vector.scalar_tensor_tensor(acc[d % 2][:], ee[:], val_col[:, d : d + 1], acc[d % 2][:], MULT, ADD)
+        for i in range(2):
+            for b in range(4):
+                nc.tensor.matmul(
+                    num[:, b, :], acc[i][:, P * b : P * (b + 1)], ident[:],
+                    is_transpose=True, start=(i == 0 and b == 0), stop=(i == 1 and b == 3),
+                )
+        out_rows = out.rearrange("(b p) v -> p b v", p=P)
+        rec = [keep.tile([P, 2, V], F32, name="rec%d" % g) for g in range(2)]
+        nc.vector.reciprocal(rec[0][:], den[0][:])
+        root = keep.tile([P, 2, V], F32, name="root")
+        nc.scalar.activation(root[:], den[1][:], RSQRT)
+        nc.scalar.activation(rec[1][:], root[:], SQUARE)
+        for g in range(2):
+            res = keep.tile([P, 2, V], F32, name="res%d" % g)
+            nc.vector.tensor_tensor(res[:], num[:, 2 * g : 2 * g + 2, :], rec[g][:], MULT)
+            nc.sync.dma_start(out_rows[:, 2 * g : 2 * g + 2, :], res[:])

@@ -29,8 +29,7 @@ def tile_picked_ynw_avg_p_kernel(
     nc = tc.nc
     with ExitStack() as ctx:
         keep = ctx.enter_context(tc.tile_pool(name="keep", bufs=1))
-        shared = ctx.enter_context(tc.tile_pool(name="shared", bufs=1))
-        banks = ctx.enter_context(tc.psum_pool(name="banks", bufs=5))
+        banks = ctx.enter_context(tc.psum_pool(name="banks", bufs=7))
         sums = ctx.enter_context(tc.psum_pool(name="sums", bufs=1))
 
         ex_list = keep.tile([P, U // 16], U16, name="ex_list")
@@ -39,152 +38,160 @@ def tile_picked_ynw_avg_p_kernel(
         val_win = keep.tile([P, W], F32, name="val_win")
         es_win = keep.tile([P, W], U8, name="es_win")
         xs_win = keep.tile([P, T], U8, name="xs_win")
-        ew_win = keep.tile([P, W], I32, name="ew_win")
-        xw_win = [keep.tile([P, T], I32, name="xw_win%d" % o) for o in range(PASSES)]
-        w_raw = [[keep.tile([P, 4, H // 2], F32, name="w_raw%d%d" % (o, u)) for u in range(2)] for o in range(PASSES)]
+        w_raw = [keep.tile([P, 4, H], F32, name="w_raw%d" % o) for o in range(PASSES)]
 
         zero = keep.tile([P, 1], F32, name="zero")
-        nc.vector.memset(zero[:], 0.0)
         nc.vector.memset(xs_win[:].bitcast(I32), 0)
-        nc.vector.memset(es_win[:].bitcast(I32), 0)
+        nc.vector.memset(zero[:], 0.0)
         nc.vector.memset(half_win[0 : P - 1, :], 0.0)
-        nc.scalar.copy(val_win[0 : P - 1, :], zero[0 : P - 1, :].to_broadcast([P - 1, W]))
+        nc.scalar.copy(val_win[:], zero[:].to_broadcast([P, W]))
 
-        def load_w(o, u):
-            rows = w1[o * 512 : (o + 1) * 512, u * (H // 2) : (u + 1) * (H // 2)]
-            nc.sync.dma_start(w_raw[o][u][:], rows.rearrange("(p j) c -> p j c", j=4))
+        xw_win = [keep.tile([P, T], I32, name="xw_win%d" % o) for o in range(PASSES)]
+        ew_win = keep.tile([P, W], I32, name="ew_win")
+
+        def load_w(o):
+            nc.sync.dma_start(w_raw[o][:], w1[o * 512 : (o + 1) * 512, :].rearrange("(p j) c -> p j c", j=4))
 
         nc.sync.dma_start(ex_list[:], ex)
-        nc.sync.dma_start(half_win[P - 1 : P, :], half[0:1, :])
-        nc.sync.dma_start(val_win[P - 1 : P, :], val[0:1, :])
+        nc.scalar.dma_start(half_win[P - 1 : P, :], half[0:1, :])
         nc.sync.dma_start(offs_list[:], offs)
-        for o in range(PASSES):
-            nc.sync.dma_start(xw_win[o][:], x_words[o].rearrange("p n t -> p (n t)").bitcast(I32))
+        for q in range(4):
+            rows = e_scales[0:1, 4 * q : 4 * q + 4, :].bitcast(I32).broadcast_to([8, 4, W // 4])
+            nc.sync.dma_start(es_win[32 * q : 32 * q + 32, :].bitcast(I32), rows)
+        load_w(0)
         for q in range(4):
             nc.sync.dma_start(xs_win[32 * q : 32 * q + 8, :].bitcast(I32), x_scales[:, 4 * q : 4 * q + 4, :].bitcast(I32))
+        load_w(1)
         for o in range(PASSES):
-            for u in range(2):
-                load_w(o, u)
+            nc.sync.dma_start(xw_win[o][:], x_words[o].rearrange("p n t -> p (n t)").bitcast(I32))
         nc.sync.dma_start(ew_win[:], e_words[0].rearrange("p n t -> p (n t)").bitcast(I32))
-        for q in range(4):
-            nc.sync.dma_start(es_win[32 * q : 32 * q + 4, :].bitcast(I32), e_scales[0, 4 * q : 4 * q + 4, :].bitcast(I32))
+        nc.sync.dma_start(val_win[P - 1 : P, :], val[0:1, :])
 
         ident = keep.tile([P, P], F32, name="ident")
         make_identity(nc, ident[:])
 
         half_ex = keep.tile([P, U], F32, name="half_ex")
-        val_ex = keep.tile([P, U], F32, name="val_ex")
         nc.vector.tensor_copy(half_ex[:], half_win[:].indirect(ex_list[:]))
-        nc.vector.tensor_copy(val_ex[:], val_win[:].indirect(ex_list[:]))
-        half_col = keep.tile([P, D], F32, name="half_col")
-        val_col = keep.tile([P, D], F32, name="val_col")
-        nc.gpsimd.dma_start(half_col[:], half_ex[P - 1 : P, :].rearrange("o (v d) -> o v d", d=D))
-        nc.gpsimd.dma_start(val_col[:], val_ex[P - 1 : P, :].rearrange("o (v d) -> o v d", d=D))
-        neg_half = keep.tile([P, D], F32, name="neg_half")
-        nc.gpsimd.tensor_scalar(neg_half[:], half_col[:], -1.0, 0.0, MULT, ADD)
+        es_ex = keep.tile([P, U], U8, name="es_ex")
+        nc.vector.tensor_copy(es_ex[:], es_win[:].indirect(ex_list[:]))
 
-        xw = []
-        for o in range(PASSES):
-            words = keep.tile([P, S], U32, name="xw%d" % o, align_bytes=64)
-            nc.vector.tensor_copy(words[:], xw_win[o][:].bitcast(U32).indirect(offs_list[:]))
-            xw.append(words)
-        xs = keep.tile([P, S], U8, name="xs", align_bytes=64)
-        nc.vector.tensor_copy(xs[:], xs_win[:].indirect(offs_list[:]))
-
-        w_codes = []
-        w_scales = []
-        for o in range(PASSES):
+        def quantize_w(o):
             w_bf = keep.tile([P, 4 * H], BF16, name="w_bf%d" % o, align_bytes=64)
-            dst = w_bf[:].rearrange("p (t m j) -> p m t j", t=4, j=4)
-            for u in range(2):
-                nc.scalar.copy(dst[:, 64 * u : 64 * (u + 1), :, :], w_raw[o][u][:].rearrange("p j (m t) -> p m t j", t=4))
+            nc.scalar.copy(
+                w_bf[:].rearrange("p (t m j) -> p m j t", t=4, j=4), w_raw[o][:].rearrange("p j (m t) -> p m j t", t=4)
+            )
             codes = keep.tile([P, H], U32, name="w_codes%d" % o, align_bytes=64)
             scales = keep.tile([P, H], U8, name="w_scales%d" % o, align_bytes=64)
             nc.vector.quantize_mx(codes[:].bitcast(FP8X4), scales[:], w_bf[:])
-            w_codes.append(codes)
-            w_scales.append(scales)
+            return codes, scales
+
+        xs = keep.tile([P, S], U8, name="xs", align_bytes=64)
+        nc.vector.tensor_copy(xs[:], xs_win[:].indirect(offs_list[:]))
+        w_mx = []
+        xw = []
+        for o in range(PASSES):
+            w_mx.append(quantize_w(o))
+            words = keep.tile([P, S], U32, name="xw%d" % o, align_bytes=64)
+            nc.vector.tensor_copy(words[:], xw_win[o][:].bitcast(U32).indirect(offs_list[:]))
+            xw.append(words)
+        w_codes = [codes for codes, scales in w_mx]
+        w_scales = [scales for codes, scales in w_mx]
+
+        half_col = keep.tile([P, D], F32, name="half_col", tag="w_raw1")
+        nc.sync.dma_start(half_col[:], half_ex[P - 1 : P, :].rearrange("o (v d) -> o v d", d=D))
+        neg_half = keep.tile([P, D], F32, name="neg_half")
+        nc.scalar.mul(neg_half[:], half_col[:], -1.0)
 
         ew_ex = keep.tile([P, U], U32, name="ew_ex")
-        es_ex = keep.tile([P, U], U8, name="es_ex")
         nc.vector.tensor_copy(ew_ex[:], ew_win[:].bitcast(U32).indirect(ex_list[:]))
-        nc.vector.tensor_copy(es_ex[:], es_win[:].indirect(ex_list[:]))
 
-        h_bf = shared.tile([P, S, 4], BF16, name="h_bf", align_bytes=64, offset=0)
+        h_bf = keep.tile([P, S, 4], BF16, name="h_bf", align_bytes=64)
         h_codes = keep.tile([P, S], U32, name="h_codes", align_bytes=64)
         h_scales = keep.tile([P, S], U8, name="h_scales", align_bytes=64)
-        for b in range(4):
-            cols = slice(P * b, P * (b + 1))
-            h_ps = banks.tile([P, 4, P], F32, name="h_ps", tag="bank")
-            for t in range(4):
-                for o in range(PASSES):
+        h_ps = [banks.tile([P, 4, P], F32, name="h_ps%d" % b, tag="bank") for b in range(4)]
+        for o in range(PASSES):
+            for b in range(4):
+                cols = slice(P * b, P * (b + 1))
+                for t in range(4):
                     nc.tensor.matmul_mx(
-                        h_ps[:, t, :],
+                        h_ps[b][:, t, :],
                         lhsT=w_codes[o][:, P * t : P * (t + 1)].bitcast(FP8X4),
                         lhsT_scale=w_scales[o][:, P * t : P * (t + 1)],
                         rhs=xw[o][:, cols].bitcast(FP8X4),
                         rhs_scale=xs[4 * o : P, cols],
-                        start=(o == 0),
-                        stop=(o == PASSES - 1),
+                        start=(o == 0 and t == 0),
+                        stop=(o == PASSES - 1 and t == 3),
                     )
-            nc.scalar.copy(h_bf[:, cols, :], h_ps[:].rearrange("p t n -> p n t"))
+                if o == PASSES - 1:
+                    nc.scalar.copy(h_bf[:, cols, :], h_ps[b][:].rearrange("p t n -> p n t"))
 
-        def deal(a, codes, scales):
-            nc.vector.tensor_copy(
-                codes[:].rearrange("p (b vq vl) -> p vq b vl", b=4, vl=4),
-                ew_ex[:].rearrange("p (vq vl a b) -> p a vq b vl", a=2, b=4, vl=4)[:, a],
-            )
-            nc.vector.tensor_copy(
-                scales[:].rearrange("p (b v) -> p v b", b=4),
-                es_ex[:].rearrange("p (v a b) -> p a v b", a=2, b=4)[:, a],
-            )
-
-        e_codes = [keep.tile([P, U // 2], U32, name="e_codes0", align_bytes=64)]
-        e_bytes = [keep.tile([P, U // 2], U8, name="e_bytes0", align_bytes=64)]
-        deal(0, e_codes[0], e_bytes[0])
+        e_codes = keep.tile([P, U], U32, name="e_codes", align_bytes=64)
+        e_bytes = keep.tile([P, U], U8, name="e_bytes", tag="w_bf1", align_bytes=64)
+        nc.vector.tensor_copy(
+            e_bytes[:].rearrange("p (a b v) -> p a v b", a=2, b=4), es_ex[:].rearrange("p (v a b) -> p a v b", a=2, b=4)
+        )
+        nc.vector.tensor_copy(
+            e_codes[:].rearrange("p (a b vq vl) -> p a vq b vl", a=2, b=4, vl=4),
+            ew_ex[:].rearrange("p (vq vl a b) -> p a vq b vl", a=2, b=4, vl=4),
+        )
         nc.vector.quantize_mx(h_codes[:].bitcast(FP8X4), h_scales[:], h_bf[:].rearrange("p n t -> p (n t)"))
-        e_codes.append(shared.tile([P, U // 2], U32, name="e_codes1", align_bytes=64, offset=0))
-        e_bytes.append(shared.tile([P, U // 2], U8, name="e_bytes1", align_bytes=64, offset=2048))
-        deal(1, e_codes[1], e_bytes[1])
 
-        den = [sums.tile([P, 2, V], F32, name="den%d" % g) for g in range(2)]
-        num = sums.tile([P, 4, V], F32, name="num")
-        acc = [keep.tile([P, S], F32, name="acc%d" % i) for i in range(2)]
+        val_ex = keep.tile([P, U], F32, name="val_ex", tag="h_bf", align_bytes=64)
+        nc.vector.tensor_copy(val_ex[:], val_win[:].indirect(ex_list[:]))
+        val_col = keep.tile([P, D], F32, name="val_col")
+        nc.sync.dma_start(val_col[:], val_ex[P - 1 : P, :].rearrange("o (v d) -> o v d", d=D))
+
+        ee = [keep.tile([P, S], F32, name="ee%d" % d) for d in range(D)]
         for d in range(D):
             y_ps = banks.tile([P, S], F32, name="y_ps", tag="bank")
-            cols = slice(V * (d % 4), V * (d % 4 + 1))
+            cols = slice(V * d, V * (d + 1))
             nc.tensor.matmul_mx(
                 y_ps[:],
-                lhsT=e_codes[d // 4][:, cols].bitcast(FP8X4),
-                lhsT_scale=e_bytes[d // 4][:, cols],
+                lhsT=e_codes[:, cols].bitcast(FP8X4),
+                lhsT_scale=e_bytes[:, cols],
                 rhs=h_codes[:].bitcast(FP8X4),
                 rhs_scale=h_scales[:],
                 start=True,
                 stop=True,
             )
-            ee = keep.tile([P, S], F32, name="ee%d" % d)
-            nc.scalar.activation(ee[:], y_ps[:], EXP, bias=neg_half[:, d : d + 1], scale=0.5)
+            nc.scalar.activation(ee[d][:], y_ps[:], EXP, bias=neg_half[:, d : d + 1], scale=0.5)
+        table_warm = keep.tile([P, 1], F32, name="table_warm")
+        nc.scalar.activation(table_warm[:], ee[D - 1][:, 0:1], RSQRT)
+        pair = [keep.tile([P, S], F32, name="pair%d" % i) for i in range(2)]
+        for i in range(2):
+            nc.vector.tensor_tensor(pair[i][:], ee[2 * i][:], ee[2 * i + 1][:], ADD)
+        first_four = keep.tile([P, S], F32, name="first_four")
+        nc.vector.tensor_tensor(first_four[:], pair[0][:], pair[1][:], ADD)
+        den = sums.tile([P, 4, V], F32, name="den")
+        den_terms = [first_four] + ee[4:]
+        for i, term in enumerate(den_terms):
             for b in range(4):
                 nc.tensor.matmul(
-                    den[b // 2][:, b % 2, :], ee[:, P * b : P * (b + 1)], ident[:],
-                    is_transpose=True, start=(d == 0 and b % 2 == 0), stop=(d == D - 1 and b % 2 == 1),
+                    den[:, b, :], term[:, P * b : P * (b + 1)], ident[:],
+                    is_transpose=True, start=(i == 0 and b == 0), stop=(i == len(den_terms) - 1 and b == 3),
                 )
-            if d < 2:
-                nc.vector.tensor_scalar(acc[d][:], ee[:], val_col[:, d : d + 1], None, MULT)
-            else:
-                nc.vector.scalar_tensor_tensor(acc[d % 2][:], ee[:], val_col[:, d : d + 1], acc[d % 2][:], MULT, ADD)
+        root = keep.tile([P, 4, V], F32, name="root")
+        rec = keep.tile([P, 4, V], F32, name="rec")
+        nc.scalar.activation(root[:], den[:], RSQRT)
+        nc.scalar.activation(rec[:], root[:], SQUARE)
+
+        acc = [keep.tile([P, S], F32, name="acc%d" % i, tag="pair%d" % i) for i in range(2)]
+        for d in range(2):
+            nc.vector.tensor_scalar(acc[d][:], ee[d][:], val_col[:, d : d + 1], None, MULT)
+        for d in range(2, D - 1):
+            nc.vector.scalar_tensor_tensor(acc[d % 2][:], ee[d][:], val_col[:, d : d + 1], acc[d % 2][:], MULT, ADD)
+        for g in range(2):
+            cols = slice(256 * g, 256 * (g + 1))
+            nc.vector.scalar_tensor_tensor(acc[1][:, cols], ee[D - 1][:, cols], val_col[:, D - 1 : D], acc[1][:, cols], MULT, ADD)
+        num = [banks.tile([P, 2, V], F32, name="num%d" % g, tag="bank") for g in range(2)]
         for i in range(2):
             for b in range(4):
                 nc.tensor.matmul(
-                    num[:, b, :], acc[i][:, P * b : P * (b + 1)], ident[:],
-                    is_transpose=True, start=(i == 0 and b == 0), stop=(i == 1 and b == 3),
+                    num[b // 2][:, b % 2, :], acc[i][:, P * b : P * (b + 1)], ident[:],
+                    is_transpose=True, start=(i == 0 and b % 2 == 0), stop=(i == 1 and b % 2 == 1),
                 )
         out_rows = out.rearrange("(b p) v -> p b v", p=P)
-        rec = [keep.tile([P, 2, V], F32, name="rec%d" % g) for g in range(2)]
-        nc.vector.reciprocal(rec[0][:], den[0][:])
-        root = keep.tile([P, 2, V], F32, name="root")
-        nc.scalar.activation(root[:], den[1][:], RSQRT)
-        nc.scalar.activation(rec[1][:], root[:], SQUARE)
         for g in range(2):
             res = keep.tile([P, 2, V], F32, name="res%d" % g)
-            nc.vector.tensor_tensor(res[:], num[:, 2 * g : 2 * g + 2, :], rec[g][:], MULT)
+            nc.vector.tensor_tensor(res[:], num[g][:], rec[:, 2 * g : 2 * g + 2, :], MULT)
             nc.sync.dma_start(out_rows[:, 2 * g : 2 * g + 2, :], res[:])

@@ -17,9 +17,24 @@ RSQRT = mybir.ActivationFunctionType.Abs_reciprocal_sqrt
 SQUARE = mybir.ActivationFunctionType.Square
 
 P = 128
-K, T, S, H, D, W, U = 1024, 1024, 512, 512, 8, 2048, 1024
+PACK = 4
+K = 1024
+T = 1024
+S = 512
+H = 512
+W = 2048
+U = 1024
+D = 8
 V = U // D
-PASSES = K // 512
+PASS_ROWS = P * PACK
+PASSES = K // PASS_ROWS
+QUADRANT = 32
+QUADRANTS = P // QUADRANT
+BLOCKS = S // P
+PARTS = 2
+PART_BLOCKS = BLOCKS // PARTS
+LAST = P - 1
+WORK_BANKS = 7
 FLOPS = 2 * K * H * S + 2 * H * S * U
 
 
@@ -29,7 +44,8 @@ def tile_picked_ynw_avg_p_kernel(
     nc = tc.nc
     with ExitStack() as ctx:
         keep = ctx.enter_context(tc.tile_pool(name="keep", bufs=1))
-        banks = ctx.enter_context(tc.psum_pool(name="banks", bufs=7))
+        partial = ctx.enter_context(tc.tile_pool(name="partial", bufs=1))
+        banks = ctx.enter_context(tc.psum_pool(name="banks", bufs=WORK_BANKS))
         sums = ctx.enter_context(tc.psum_pool(name="sums", bufs=1))
 
         ex_list = keep.tile([P, U // 16], U16, name="ex_list")
@@ -38,34 +54,38 @@ def tile_picked_ynw_avg_p_kernel(
         val_win = keep.tile([P, W], F32, name="val_win")
         es_win = keep.tile([P, W], U8, name="es_win")
         xs_win = keep.tile([P, T], U8, name="xs_win")
-        w_raw = [keep.tile([P, 4, H], F32, name="w_raw%d" % o) for o in range(PASSES)]
+        w_raw = [keep.tile([P, PACK, H], F32, name="w_raw%d" % o) for o in range(PASSES)]
 
         zero = keep.tile([P, 1], F32, name="zero")
         nc.vector.memset(xs_win[:].bitcast(I32), 0)
         nc.vector.memset(zero[:], 0.0)
-        nc.vector.memset(half_win[0 : P - 1, :], 0.0)
+        nc.vector.memset(half_win[0:LAST, :], 0.0)
         nc.scalar.copy(val_win[:], zero[:].to_broadcast([P, W]))
 
-        xw_win = [keep.tile([P, T], I32, name="xw_win%d" % o) for o in range(PASSES)]
+        xw_win = [keep.tile([P, T], I32, name="xw_win%d" % o, align_bytes=64) for o in range(PASSES)]
         ew_win = keep.tile([P, W], I32, name="ew_win")
 
         def load_w(o):
-            nc.sync.dma_start(w_raw[o][:], w1[o * 512 : (o + 1) * 512, :].rearrange("(p j) c -> p j c", j=4))
+            rows = w1[o * PASS_ROWS : (o + 1) * PASS_ROWS, :]
+            nc.sync.dma_start(w_raw[o][:], rows.rearrange("(p j) c -> p j c", j=PACK))
 
         nc.sync.dma_start(ex_list[:], ex)
-        nc.scalar.dma_start(half_win[P - 1 : P, :], half[0:1, :])
+        nc.scalar.dma_start(half_win[LAST:P, :], half[0:1, :])
         nc.sync.dma_start(offs_list[:], offs)
-        for q in range(4):
-            rows = e_scales[0:1, 4 * q : 4 * q + 4, :].bitcast(I32).broadcast_to([8, 4, W // 4])
-            nc.sync.dma_start(es_win[32 * q : 32 * q + 32, :].bitcast(I32), rows)
+        for q in range(QUADRANTS):
+            scale_rows = e_scales[0:1, 4 * q : 4 * q + 4, :].bitcast(I32).broadcast_to([QUADRANT // 4, 4, W // 4])
+            nc.sync.dma_start(es_win[QUADRANT * q : QUADRANT * (q + 1), :].bitcast(I32), scale_rows)
         load_w(0)
-        for q in range(4):
-            nc.sync.dma_start(xs_win[32 * q : 32 * q + 8, :].bitcast(I32), x_scales[:, 4 * q : 4 * q + 4, :].bitcast(I32))
+        for q in range(QUADRANTS):
+            nc.sync.dma_start(
+                xs_win[QUADRANT * q : QUADRANT * q + 4 * PASSES, :].bitcast(I32),
+                x_scales[:, 4 * q : 4 * q + 4, :].bitcast(I32),
+            )
         load_w(1)
         for o in range(PASSES):
-            nc.sync.dma_start(xw_win[o][:], x_words[o].rearrange("p n t -> p (n t)").bitcast(I32))
-        nc.sync.dma_start(ew_win[:], e_words[0].rearrange("p n t -> p (n t)").bitcast(I32))
-        nc.sync.dma_start(val_win[P - 1 : P, :], val[0:1, :])
+            nc.sync.dma_start(xw_win[o][:], x_words[o].rearrange("p n j -> p (n j)").bitcast(I32))
+        nc.sync.dma_start(ew_win[:], e_words[0].rearrange("p n j -> p (n j)").bitcast(I32))
+        nc.sync.dma_start(val_win[LAST:P, :], val[0:1, :])
 
         ident = keep.tile([P, P], F32, name="ident")
         make_identity(nc, ident[:])
@@ -76,9 +96,10 @@ def tile_picked_ynw_avg_p_kernel(
         nc.vector.tensor_copy(es_ex[:], es_win[:].indirect(ex_list[:]))
 
         def quantize_w(o):
-            w_bf = keep.tile([P, 4 * H], BF16, name="w_bf%d" % o, align_bytes=64)
+            w_bf = keep.tile([P, PACK * H], BF16, name="w_bf%d" % o, align_bytes=64)
             nc.scalar.copy(
-                w_bf[:].rearrange("p (t m j) -> p m j t", t=4, j=4), w_raw[o][:].rearrange("p j (m t) -> p m j t", t=4)
+                w_bf[:].rearrange("p (t m j) -> p m j t", t=PACK, j=PACK),
+                w_raw[o][:].rearrange("p j (m t) -> p m j t", t=PACK),
             )
             codes = keep.tile([P, H], U32, name="w_codes%d" % o, align_bytes=64)
             scales = keep.tile([P, H], U8, name="w_scales%d" % o, align_bytes=64)
@@ -94,104 +115,125 @@ def tile_picked_ynw_avg_p_kernel(
             words = keep.tile([P, S], U32, name="xw%d" % o, align_bytes=64)
             nc.vector.tensor_copy(words[:], xw_win[o][:].bitcast(U32).indirect(offs_list[:]))
             xw.append(words)
-        w_codes = [codes for codes, scales in w_mx]
-        w_scales = [scales for codes, scales in w_mx]
 
         half_col = keep.tile([P, D], F32, name="half_col", tag="w_raw1")
-        nc.sync.dma_start(half_col[:], half_ex[P - 1 : P, :].rearrange("o (v d) -> o v d", d=D))
+        nc.sync.dma_start(half_col[:], half_ex[LAST:P, :].rearrange("r (v d) -> r v d", d=D))
         neg_half = keep.tile([P, D], F32, name="neg_half")
         nc.scalar.mul(neg_half[:], half_col[:], -1.0)
 
+        val_col = keep.tile([P, D], F32, name="val_col")
+
+        def look_up_val(u, earlier_tile):
+            val_ex = keep.tile([P, U // 2], F32, name="val_ex%d" % u, tag=earlier_tile, align_bytes=64)
+            nc.vector.tensor_copy(val_ex[:], val_win[:].indirect(ex_list[:, u * U // 32 : (u + 1) * U // 32]))
+            nc.sync.dma_start(
+                val_col[u * V // 2 : (u + 1) * V // 2, :], val_ex[LAST:P, :].rearrange("r (v d) -> r v d", d=D)
+            )
+
+        look_up_val(0, "xw_win1")
         ew_ex = keep.tile([P, U], U32, name="ew_ex")
         nc.vector.tensor_copy(ew_ex[:], ew_win[:].bitcast(U32).indirect(ex_list[:]))
 
-        h_bf = keep.tile([P, S, 4], BF16, name="h_bf", align_bytes=64)
+        h_bf = keep.tile([P, S, PACK], BF16, name="h_bf", align_bytes=64)
         h_codes = keep.tile([P, S], U32, name="h_codes", align_bytes=64)
         h_scales = keep.tile([P, S], U8, name="h_scales", align_bytes=64)
-        h_ps = [banks.tile([P, 4, P], F32, name="h_ps%d" % b, tag="bank") for b in range(4)]
+        h_ps = [banks.tile([P, PACK, P], F32, name="h_ps%d" % b, tag="bank") for b in range(BLOCKS)]
         for o in range(PASSES):
-            for b in range(4):
-                cols = slice(P * b, P * (b + 1))
-                for t in range(4):
+            w_codes, w_scales = w_mx[o]
+            for b in range(BLOCKS):
+                queries = slice(P * b, P * (b + 1))
+                for t in range(PACK):
                     nc.tensor.matmul_mx(
                         h_ps[b][:, t, :],
-                        lhsT=w_codes[o][:, P * t : P * (t + 1)].bitcast(FP8X4),
-                        lhsT_scale=w_scales[o][:, P * t : P * (t + 1)],
-                        rhs=xw[o][:, cols].bitcast(FP8X4),
-                        rhs_scale=xs[4 * o : P, cols],
+                        lhsT=w_codes[:, P * t : P * (t + 1)].bitcast(FP8X4),
+                        lhsT_scale=w_scales[:, P * t : P * (t + 1)],
+                        rhs=xw[o][:, queries].bitcast(FP8X4),
+                        rhs_scale=xs[4 * o : P, queries],
                         start=(o == 0 and t == 0),
-                        stop=(o == PASSES - 1 and t == 3),
+                        stop=(o == PASSES - 1 and t == PACK - 1),
                     )
                 if o == PASSES - 1:
-                    nc.scalar.copy(h_bf[:, cols, :], h_ps[b][:].rearrange("p t n -> p n t"))
+                    nc.scalar.copy(h_bf[:, queries, :], h_ps[b][:].rearrange("p t n -> p n t"))
 
         e_codes = keep.tile([P, U], U32, name="e_codes", align_bytes=64)
         e_bytes = keep.tile([P, U], U8, name="e_bytes", tag="w_bf1", align_bytes=64)
         nc.vector.tensor_copy(
-            e_bytes[:].rearrange("p (a b v) -> p a v b", a=2, b=4), es_ex[:].rearrange("p (v a b) -> p a v b", a=2, b=4)
+            e_bytes[:].rearrange("p (a c v) -> p a v c", a=2, c=4),
+            es_ex[:].rearrange("p (v a c) -> p a v c", a=2, c=4),
         )
         nc.vector.tensor_copy(
-            e_codes[:].rearrange("p (a b vq vl) -> p a vq b vl", a=2, b=4, vl=4),
-            ew_ex[:].rearrange("p (vq vl a b) -> p a vq b vl", a=2, b=4, vl=4),
+            e_codes[:].rearrange("p (a c vq vl) -> p a vq c vl", a=2, c=4, vl=4),
+            ew_ex[:].rearrange("p (vq vl a c) -> p a vq c vl", a=2, c=4, vl=4),
         )
         nc.vector.quantize_mx(h_codes[:].bitcast(FP8X4), h_scales[:], h_bf[:].rearrange("p n t -> p (n t)"))
 
-        val_ex = keep.tile([P, U], F32, name="val_ex", tag="h_bf", align_bytes=64)
-        nc.vector.tensor_copy(val_ex[:], val_win[:].indirect(ex_list[:]))
-        val_col = keep.tile([P, D], F32, name="val_col")
-        nc.sync.dma_start(val_col[:], val_ex[P - 1 : P, :].rearrange("o (v d) -> o v d", d=D))
+        look_up_val(1, "h_bf")
 
         ee = [keep.tile([P, S], F32, name="ee%d" % d) for d in range(D)]
         for d in range(D):
             y_ps = banks.tile([P, S], F32, name="y_ps", tag="bank")
-            cols = slice(V * d, V * (d + 1))
+            member = slice(V * d, V * (d + 1))
             nc.tensor.matmul_mx(
                 y_ps[:],
-                lhsT=e_codes[:, cols].bitcast(FP8X4),
-                lhsT_scale=e_bytes[:, cols],
+                lhsT=e_codes[:, member].bitcast(FP8X4),
+                lhsT_scale=e_bytes[:, member],
                 rhs=h_codes[:].bitcast(FP8X4),
                 rhs_scale=h_scales[:],
                 start=True,
                 stop=True,
             )
             nc.scalar.activation(ee[d][:], y_ps[:], EXP, bias=neg_half[:, d : d + 1], scale=0.5)
+
         table_warm = keep.tile([P, 1], F32, name="table_warm")
         nc.scalar.activation(table_warm[:], ee[D - 1][:, 0:1], RSQRT)
-        pair = [keep.tile([P, S], F32, name="pair%d" % i) for i in range(2)]
-        for i in range(2):
-            nc.vector.tensor_tensor(pair[i][:], ee[2 * i][:], ee[2 * i + 1][:], ADD)
-        first_four = keep.tile([P, S], F32, name="first_four")
-        nc.vector.tensor_tensor(first_four[:], pair[0][:], pair[1][:], ADD)
-        den = sums.tile([P, 4, V], F32, name="den")
-        den_terms = [first_four] + ee[4:]
-        for i, term in enumerate(den_terms):
-            for b in range(4):
-                nc.tensor.matmul(
-                    den[:, b, :], term[:, P * b : P * (b + 1)], ident[:],
-                    is_transpose=True, start=(i == 0 and b == 0), stop=(i == len(den_terms) - 1 and b == 3),
-                )
-        root = keep.tile([P, 4, V], F32, name="root")
-        rec = keep.tile([P, 4, V], F32, name="rec")
-        nc.scalar.activation(root[:], den[:], RSQRT)
-        nc.scalar.activation(rec[:], root[:], SQUARE)
 
-        acc = [keep.tile([P, S], F32, name="acc%d" % i, tag="pair%d" % i) for i in range(2)]
+        first_two = partial.tile([P, S], F32, name="first_two", offset=2 * S)
+        nc.vector.tensor_tensor(first_two[:], ee[0][:], ee[1][:], ADD)
+        first_three = keep.tile([P, S], F32, name="first_three")
+        nc.vector.tensor_tensor(first_three[:], first_two[:], ee[2][:], ADD)
+        den = sums.tile([P, BLOCKS, V], F32, name="den")
+        den_terms = [first_three] + ee[3:]
+        for i, term in enumerate(den_terms):
+            for b in range(BLOCKS):
+                nc.tensor.matmul(
+                    den[:, b, :],
+                    term[:, P * b : P * (b + 1)],
+                    ident[:],
+                    is_transpose=True,
+                    start=(i == 0 and b == 0),
+                    stop=(i == len(den_terms) - 1 and b == BLOCKS - 1),
+                )
+
+        rec = [keep.tile([P, PART_BLOCKS, V], F32, name="rec%d" % g) for g in range(PARTS)]
+        for g in range(PARTS):
+            root = keep.tile([P, PART_BLOCKS, V], F32, name="root%d" % g)
+            nc.scalar.activation(root[:], den[:, PART_BLOCKS * g : PART_BLOCKS * (g + 1), :], RSQRT)
+            nc.scalar.activation(rec[g][:], root[:], SQUARE)
+
+        acc = [partial.tile([P, S], F32, name="acc%d" % i, offset=4 * S * i) for i in range(2)]
         for d in range(2):
             nc.vector.tensor_scalar(acc[d][:], ee[d][:], val_col[:, d : d + 1], None, MULT)
         for d in range(2, D - 1):
             nc.vector.scalar_tensor_tensor(acc[d % 2][:], ee[d][:], val_col[:, d : d + 1], acc[d % 2][:], MULT, ADD)
-        for g in range(2):
-            cols = slice(256 * g, 256 * (g + 1))
-            nc.vector.scalar_tensor_tensor(acc[1][:, cols], ee[D - 1][:, cols], val_col[:, D - 1 : D], acc[1][:, cols], MULT, ADD)
-        num = [banks.tile([P, 2, V], F32, name="num%d" % g, tag="bank") for g in range(2)]
+        for g in range(PARTS):
+            part = slice(P * PART_BLOCKS * g, P * PART_BLOCKS * (g + 1))
+            nc.vector.scalar_tensor_tensor(
+                acc[1][:, part], ee[D - 1][:, part], val_col[:, D - 1 : D], acc[1][:, part], MULT, ADD
+            )
+        num = [banks.tile([P, PART_BLOCKS, V], F32, name="num%d" % g, tag="bank") for g in range(PARTS)]
         for i in range(2):
-            for b in range(4):
+            for b in range(BLOCKS):
                 nc.tensor.matmul(
-                    num[b // 2][:, b % 2, :], acc[i][:, P * b : P * (b + 1)], ident[:],
-                    is_transpose=True, start=(i == 0 and b % 2 == 0), stop=(i == 1 and b % 2 == 1),
+                    num[b // PART_BLOCKS][:, b % PART_BLOCKS, :],
+                    acc[i][:, P * b : P * (b + 1)],
+                    ident[:],
+                    is_transpose=True,
+                    start=(i == 0 and b % PART_BLOCKS == 0),
+                    stop=(i == 1 and b % PART_BLOCKS == PART_BLOCKS - 1),
                 )
+
         out_rows = out.rearrange("(b p) v -> p b v", p=P)
-        for g in range(2):
-            res = keep.tile([P, 2, V], F32, name="res%d" % g)
-            nc.vector.tensor_tensor(res[:], num[g][:], rec[:, 2 * g : 2 * g + 2, :], MULT)
-            nc.sync.dma_start(out_rows[:, 2 * g : 2 * g + 2, :], res[:])
+        for g in range(PARTS):
+            res = keep.tile([P, PART_BLOCKS, V], F32, name="res%d" % g)
+            nc.vector.tensor_tensor(res[:], num[g][:], rec[g][:], MULT)
+            nc.sync.dma_start(out_rows[:, PART_BLOCKS * g : PART_BLOCKS * (g + 1), :], res[:])

@@ -33,8 +33,9 @@ QUADRANTS = P // QUADRANT
 BLOCKS = S // P
 PARTS = 2
 PART_BLOCKS = BLOCKS // PARTS
-LAST = P - 1
-WORK_BANKS = 7
+HALF_ROW = P - 2
+VAL_ROW = P - 1
+BANKS = 8
 FLOPS = 2 * K * H * S + 2 * H * S * U
 
 
@@ -44,97 +45,99 @@ def tile_picked_ynw_avg_p_kernel(
     nc = tc.nc
     with ExitStack() as ctx:
         keep = ctx.enter_context(tc.tile_pool(name="keep", bufs=1))
-        partial = ctx.enter_context(tc.tile_pool(name="partial", bufs=1))
-        banks = ctx.enter_context(tc.psum_pool(name="banks", bufs=WORK_BANKS))
-        sums = ctx.enter_context(tc.psum_pool(name="sums", bufs=1))
+        late = ctx.enter_context(tc.tile_pool(name="late", bufs=1))
+        after_cast = ctx.enter_context(tc.tile_pool(name="after_cast", bufs=1))
+        banks = ctx.enter_context(tc.psum_pool(name="banks", bufs=BANKS))
 
         ex_list = keep.tile([P, U // 16], U16, name="ex_list")
         offs_list = keep.tile([P, S // 16], U16, name="offs_list")
-        half_win = keep.tile([P, W], F32, name="half_win")
-        val_win = keep.tile([P, W], F32, name="val_win")
-        es_win = keep.tile([P, W], U8, name="es_win")
+        hv_win = keep.tile([P, W], F32, name="hv_win")
+        es_win = keep.tile([P, W], U8, name="es_win", align_bytes=64)
         xs_win = keep.tile([P, T], U8, name="xs_win")
-        w_raw = [keep.tile([P, PACK, H], F32, name="w_raw%d" % o) for o in range(PASSES)]
+        w_raw0 = keep.tile([P, PACK, H], F32, name="w_raw0")
+        w_raw1a = keep.tile([P, PACK, H // 2], F32, name="w_raw1a")
+        w_raw1b = after_cast.tile([P, PACK, H // 2], F32, name="w_raw1b", offset=0, align_bytes=64)
+        w_pieces = [[(w_raw0, 0, H)], [(w_raw1a, 0, H // 2), (w_raw1b, H // 2, H)]]
 
-        zero = keep.tile([P, 1], F32, name="zero")
         nc.vector.memset(xs_win[:].bitcast(I32), 0)
-        nc.vector.memset(zero[:], 0.0)
-        nc.vector.memset(half_win[0:LAST, :], 0.0)
-        nc.scalar.copy(val_win[:], zero[:].to_broadcast([P, W]))
+        nc.vector.memset(hv_win[0:HALF_ROW, :], 0.0)
 
         xw_win = [keep.tile([P, T], I32, name="xw_win%d" % o, align_bytes=64) for o in range(PASSES)]
         ew_win = keep.tile([P, W], I32, name="ew_win")
 
-        def load_w(o):
-            rows = w1[o * PASS_ROWS : (o + 1) * PASS_ROWS, :]
-            nc.sync.dma_start(w_raw[o][:], rows.rearrange("(p j) c -> p j c", j=PACK))
+        def load_w(o, piece):
+            raw, first, end = w_pieces[o][piece]
+            rows = w1[o * PASS_ROWS : (o + 1) * PASS_ROWS, first:end]
+            nc.sync.dma_start(raw[:], rows.rearrange("(p j) c -> p j c", j=PACK))
 
         nc.sync.dma_start(ex_list[:], ex)
-        nc.scalar.dma_start(half_win[LAST:P, :], half[0:1, :])
-        nc.sync.dma_start(offs_list[:], offs)
+        nc.scalar.dma_start(hv_win[HALF_ROW : HALF_ROW + 1, :], half[0:1, :])
+        nc.sync.dma_start(hv_win[VAL_ROW : VAL_ROW + 1, :], val[0:1, :])
         for q in range(QUADRANTS):
             scale_rows = e_scales[0:1, 4 * q : 4 * q + 4, :].bitcast(I32).broadcast_to([QUADRANT // 4, 4, W // 4])
             nc.sync.dma_start(es_win[QUADRANT * q : QUADRANT * (q + 1), :].bitcast(I32), scale_rows)
-        load_w(0)
+        load_w(0, 0)
+        load_w(1, 0)
+        nc.sync.dma_start(offs_list[:], offs)
         for q in range(QUADRANTS):
             nc.sync.dma_start(
                 xs_win[QUADRANT * q : QUADRANT * q + 4 * PASSES, :].bitcast(I32),
                 x_scales[:, 4 * q : 4 * q + 4, :].bitcast(I32),
             )
-        load_w(1)
-        for o in range(PASSES):
-            nc.sync.dma_start(xw_win[o][:], x_words[o].rearrange("p n j -> p (n j)").bitcast(I32))
+        nc.sync.dma_start(xw_win[0][:], x_words[0].rearrange("p n j -> p (n j)").bitcast(I32))
+        load_w(1, 1)
+        nc.sync.dma_start(xw_win[1][:], x_words[1].rearrange("p n j -> p (n j)").bitcast(I32))
         nc.sync.dma_start(ew_win[:], e_words[0].rearrange("p n j -> p (n j)").bitcast(I32))
-        nc.sync.dma_start(val_win[LAST:P, :], val[0:1, :])
 
         ident = keep.tile([P, P], F32, name="ident")
         make_identity(nc, ident[:])
 
-        half_ex = keep.tile([P, U], F32, name="half_ex")
-        nc.vector.tensor_copy(half_ex[:], half_win[:].indirect(ex_list[:]))
+        hv_ex = keep.tile([P, U], F32, name="hv_ex")
+        nc.vector.tensor_copy(hv_ex[:], hv_win[:].indirect(ex_list[:]))
+
         es_ex = keep.tile([P, U], U8, name="es_ex")
         nc.vector.tensor_copy(es_ex[:], es_win[:].indirect(ex_list[:]))
 
         def quantize_w(o):
             w_bf = keep.tile([P, PACK * H], BF16, name="w_bf%d" % o, align_bytes=64)
-            nc.scalar.copy(
-                w_bf[:].rearrange("p (t m j) -> p m j t", t=PACK, j=PACK),
-                w_raw[o][:].rearrange("p j (m t) -> p m j t", t=PACK),
-            )
+            for raw, first, end in w_pieces[o]:
+                nc.scalar.copy(
+                    w_bf[:].rearrange("p (t m j) -> p m j t", t=PACK, j=PACK)[:, first // PACK : end // PACK],
+                    raw[:].rearrange("p j (m t) -> p m j t", t=PACK),
+                )
             codes = keep.tile([P, H], U32, name="w_codes%d" % o, align_bytes=64)
             scales = keep.tile([P, H], U8, name="w_scales%d" % o, align_bytes=64)
             nc.vector.quantize_mx(codes[:].bitcast(FP8X4), scales[:], w_bf[:])
             return codes, scales
 
+        w_mx = [quantize_w(0)]
         xs = keep.tile([P, S], U8, name="xs", align_bytes=64)
         nc.vector.tensor_copy(xs[:], xs_win[:].indirect(offs_list[:]))
-        w_mx = []
-        xw = []
-        for o in range(PASSES):
-            w_mx.append(quantize_w(o))
-            words = keep.tile([P, S], U32, name="xw%d" % o, align_bytes=64)
-            nc.vector.tensor_copy(words[:], xw_win[o][:].bitcast(U32).indirect(offs_list[:]))
-            xw.append(words)
+        xw0 = keep.tile([P, S], U32, name="xw0", align_bytes=64)
+        nc.vector.tensor_copy(xw0[:], xw_win[0][:].bitcast(U32).indirect(offs_list[:]))
+        w_mx.append(quantize_w(1))
+        xw = [[xw0[:, P * b : P * (b + 1)] for b in range(BLOCKS)], []]
+        for u in range(2):
+            words = after_cast.tile([P, S // 2], U32, name="xw1_%d" % u, offset=2 * S * u, align_bytes=64)
+            entries = offs_list[:, u * S // 32 : (u + 1) * S // 32]
+            nc.vector.tensor_copy(words[:], xw_win[1][:].bitcast(U32).indirect(entries))
+            xw[1].extend(words[:, P * b : P * (b + 1)] for b in range(BLOCKS // 2))
 
-        half_col = keep.tile([P, D], F32, name="half_col", tag="w_raw1")
-        nc.sync.dma_start(half_col[:], half_ex[LAST:P, :].rearrange("r (v d) -> r v d", d=D))
-        neg_half = keep.tile([P, D], F32, name="neg_half")
-        nc.scalar.mul(neg_half[:], half_col[:], -1.0)
+        hv_col = after_cast.tile([P, 2, D], F32, name="hv_col", offset=4 * S)
+        neg_half = hv_col[:, 0, :]
+        val_col = hv_col[:, 1, :]
+        for a in range(D // PACK):
+            hv_ps = banks.tile([P, PACK, P], F32, name="hv_ps", tag="bank")
+            for c in range(PACK):
+                nc.tensor.transpose(hv_ps[:, c, :], hv_ex[:, PACK * a + c : U : D], ident[:])
+            nc.scalar.mul(neg_half[:, PACK * a : PACK * (a + 1)], hv_ps[:, :, HALF_ROW], -1.0)
+            nc.scalar.copy(val_col[:, PACK * a : PACK * (a + 1)], hv_ps[:, :, VAL_ROW])
 
-        val_col = keep.tile([P, D], F32, name="val_col")
-
-        def look_up_val(u, earlier_tile):
-            val_ex = keep.tile([P, U // 2], F32, name="val_ex%d" % u, tag=earlier_tile, align_bytes=64)
-            nc.vector.tensor_copy(val_ex[:], val_win[:].indirect(ex_list[:, u * U // 32 : (u + 1) * U // 32]))
-            nc.sync.dma_start(
-                val_col[u * V // 2 : (u + 1) * V // 2, :], val_ex[LAST:P, :].rearrange("r (v d) -> r v d", d=D)
-            )
-
-        look_up_val(0, "xw_win1")
         ew_ex = keep.tile([P, U], U32, name="ew_ex")
         nc.vector.tensor_copy(ew_ex[:], ew_win[:].bitcast(U32).indirect(ex_list[:]))
 
-        h_bf = keep.tile([P, S, PACK], BF16, name="h_bf", align_bytes=64)
+
+        h_bf = late.tile([P, S, PACK], BF16, name="h_bf", offset=0, align_bytes=64)
         h_codes = keep.tile([P, S], U32, name="h_codes", align_bytes=64)
         h_scales = keep.tile([P, S], U8, name="h_scales", align_bytes=64)
         h_ps = [banks.tile([P, PACK, P], F32, name="h_ps%d" % b, tag="bank") for b in range(BLOCKS)]
@@ -147,7 +150,7 @@ def tile_picked_ynw_avg_p_kernel(
                         h_ps[b][:, t, :],
                         lhsT=w_codes[:, P * t : P * (t + 1)].bitcast(FP8X4),
                         lhsT_scale=w_scales[:, P * t : P * (t + 1)],
-                        rhs=xw[o][:, queries].bitcast(FP8X4),
+                        rhs=xw[o][b].bitcast(FP8X4),
                         rhs_scale=xs[4 * o : P, queries],
                         start=(o == 0 and t == 0),
                         stop=(o == PASSES - 1 and t == PACK - 1),
@@ -155,28 +158,34 @@ def tile_picked_ynw_avg_p_kernel(
                 if o == PASSES - 1:
                     nc.scalar.copy(h_bf[:, queries, :], h_ps[b][:].rearrange("p t n -> p n t"))
 
-        e_codes = keep.tile([P, U], U32, name="e_codes", align_bytes=64)
-        e_bytes = keep.tile([P, U], U8, name="e_bytes", tag="w_bf1", align_bytes=64)
-        nc.vector.tensor_copy(
-            e_bytes[:].rearrange("p (a c v) -> p a v c", a=2, c=4),
-            es_ex[:].rearrange("p (v a c) -> p a v c", a=2, c=4),
-        )
-        nc.vector.tensor_copy(
-            e_codes[:].rearrange("p (a c vq vl) -> p a vq c vl", a=2, c=4, vl=4),
-            ew_ex[:].rearrange("p (vq vl a c) -> p a vq c vl", a=2, c=4, vl=4),
-        )
-        nc.vector.quantize_mx(h_codes[:].bitcast(FP8X4), h_scales[:], h_bf[:].rearrange("p n t -> p (n t)"))
+        def deal(a, codes, scale_bytes):
+            nc.vector.tensor_copy(
+                scale_bytes[:].rearrange("p (c v) -> p v c", c=4),
+                es_ex[:].rearrange("p (v a c) -> p a v c", a=2, c=4)[:, a],
+            )
+            nc.vector.tensor_copy(
+                codes[:].rearrange("p (c vq vl) -> p vq c vl", c=4, vl=4),
+                ew_ex[:].rearrange("p (vq vl a c) -> p a vq c vl", a=2, c=4, vl=4)[:, a],
+            )
 
-        look_up_val(1, "h_bf")
+        e_codes0 = keep.tile([P, U // 2], U32, name="e_codes0", align_bytes=64)
+        e_bytes0 = keep.tile([P, U // 2], U8, name="e_bytes0", tag="w_bf1", align_bytes=64)
+        deal(0, e_codes0, e_bytes0)
+        nc.vector.quantize_mx(h_codes[:].bitcast(FP8X4), h_scales[:], h_bf[:].rearrange("p n t -> p (n t)"))
+        e_codes1 = late.tile([P, U // 2], U32, name="e_codes1", offset=0, align_bytes=64)
+        e_bytes1 = late.tile([P, U // 2], U8, name="e_bytes1", offset=2 * U, align_bytes=64)
+        deal(1, e_codes1, e_bytes1)
+        e_codes = [e_codes0, e_codes1]
+        e_bytes = [e_bytes0, e_bytes1]
 
         ee = [keep.tile([P, S], F32, name="ee%d" % d) for d in range(D)]
         for d in range(D):
             y_ps = banks.tile([P, S], F32, name="y_ps", tag="bank")
-            member = slice(V * d, V * (d + 1))
+            member = slice(V * (d % 4), V * (d % 4 + 1))
             nc.tensor.matmul_mx(
                 y_ps[:],
-                lhsT=e_codes[:, member].bitcast(FP8X4),
-                lhsT_scale=e_bytes[:, member],
+                lhsT=e_codes[d // 4][:, member].bitcast(FP8X4),
+                lhsT_scale=e_bytes[d // 4][:, member],
                 rhs=h_codes[:].bitcast(FP8X4),
                 rhs_scale=h_scales[:],
                 start=True,
@@ -187,53 +196,46 @@ def tile_picked_ynw_avg_p_kernel(
         table_warm = keep.tile([P, 1], F32, name="table_warm")
         nc.scalar.activation(table_warm[:], ee[D - 1][:, 0:1], RSQRT)
 
-        first_two = partial.tile([P, S], F32, name="first_two", offset=2 * S)
-        nc.vector.tensor_tensor(first_two[:], ee[0][:], ee[1][:], ADD)
-        first_three = keep.tile([P, S], F32, name="first_three")
-        nc.vector.tensor_tensor(first_three[:], first_two[:], ee[2][:], ADD)
-        den = sums.tile([P, BLOCKS, V], F32, name="den")
-        den_terms = [first_three] + ee[3:]
-        for i, term in enumerate(den_terms):
-            for b in range(BLOCKS):
-                nc.tensor.matmul(
-                    den[:, b, :],
-                    term[:, P * b : P * (b + 1)],
-                    ident[:],
-                    is_transpose=True,
-                    start=(i == 0 and b == 0),
-                    stop=(i == len(den_terms) - 1 and b == BLOCKS - 1),
-                )
-
-        rec = [keep.tile([P, PART_BLOCKS, V], F32, name="rec%d" % g) for g in range(PARTS)]
-        for g in range(PARTS):
-            root = keep.tile([P, PART_BLOCKS, V], F32, name="root%d" % g)
-            nc.scalar.activation(root[:], den[:, PART_BLOCKS * g : PART_BLOCKS * (g + 1), :], RSQRT)
-            nc.scalar.activation(rec[g][:], root[:], SQUARE)
-
-        acc = [partial.tile([P, S], F32, name="acc%d" % i, offset=4 * S * i) for i in range(2)]
+        acc = [keep.tile([P, S], F32, name="acc%d" % i) for i in range(2)]
         for d in range(2):
             nc.vector.tensor_scalar(acc[d][:], ee[d][:], val_col[:, d : d + 1], None, MULT)
+        first_two = keep.tile([P, S], F32, name="first_two")
+        nc.vector.tensor_tensor(first_two[:], ee[0][:], ee[1][:], ADD)
         for d in range(2, D - 1):
             nc.vector.scalar_tensor_tensor(acc[d % 2][:], ee[d][:], val_col[:, d : d + 1], acc[d % 2][:], MULT, ADD)
-        for g in range(PARTS):
-            part = slice(P * PART_BLOCKS * g, P * PART_BLOCKS * (g + 1))
-            nc.vector.scalar_tensor_tensor(
-                acc[1][:, part], ee[D - 1][:, part], val_col[:, D - 1 : D], acc[1][:, part], MULT, ADD
-            )
-        num = [banks.tile([P, PART_BLOCKS, V], F32, name="num%d" % g, tag="bank") for g in range(PARTS)]
-        for i in range(2):
-            for b in range(BLOCKS):
-                nc.tensor.matmul(
-                    num[b // PART_BLOCKS][:, b % PART_BLOCKS, :],
-                    acc[i][:, P * b : P * (b + 1)],
-                    ident[:],
-                    is_transpose=True,
-                    start=(i == 0 and b % PART_BLOCKS == 0),
-                    stop=(i == 1 and b % PART_BLOCKS == PART_BLOCKS - 1),
-                )
+        last = keep.tile([P, S], F32, name="last")
+        nc.vector.tensor_scalar(last[:], ee[D - 1][:], val_col[:, D - 1 : D], None, MULT)
+
+        def add_turned(dst, term, b, start, stop):
+            nc.tensor.matmul(dst, term[:, P * b : P * (b + 1)], ident[:], is_transpose=True, start=start, stop=stop)
+
+        den_v = banks.tile([P, V], F32, name="den_v", tag="bank")
+        den_s = banks.tile([P, BLOCKS - 1, V], F32, name="den_s", tag="bank")
+        num = banks.tile([P, BLOCKS, V], F32, name="num", tag="bank")
+        den_terms = [first_two] + ee[2:]
+        num_terms = {4: acc[1], 5: acc[0], 6: last}
+        for i, term in enumerate(den_terms):
+            final = i == len(den_terms) - 1
+            add_turned(den_v[:], term, 0, i == 0, final)
+            for b in range(1, BLOCKS):
+                add_turned(den_s[:, b - 1, :], term, b, i == 0 and b == 1, final and b == BLOCKS - 1)
+            if i in num_terms:
+                for b in range(BLOCKS):
+                    add_turned(num[:, b, :], num_terms[i], b, i == 4 and b == 0, final and b == BLOCKS - 1)
 
         out_rows = out.rearrange("(b p) v -> p b v", p=P)
-        for g in range(PARTS):
-            res = keep.tile([P, PART_BLOCKS, V], F32, name="res%d" % g)
-            nc.vector.tensor_tensor(res[:], num[g][:], rec[g][:], MULT)
-            nc.sync.dma_start(out_rows[:, PART_BLOCKS * g : PART_BLOCKS * (g + 1), :], res[:])
+        rec_v = keep.tile([P, V], F32, name="rec_v")
+        nc.vector.reciprocal(rec_v[:], den_v[:])
+        root = keep.tile([P, BLOCKS - 1, V], F32, name="root")
+        nc.scalar.activation(root[:], den_s[:], RSQRT)
+        rec_s = keep.tile([P, 2, V], F32, name="rec_s")
+        nc.scalar.activation(rec_s[:], root[:, 1:3, :], SQUARE)
+        once = keep.tile([P, V], F32, name="once")
+        nc.vector.tensor_tensor(once[:], num[:, 1, :], root[:, 0, :], MULT)
+        res0 = keep.tile([P, 2, V], F32, name="res0")
+        nc.vector.tensor_tensor(res0[:, 0, :], num[:, 0, :], rec_v[:], MULT)
+        nc.vector.tensor_tensor(res0[:, 1, :], once[:], root[:, 0, :], MULT)
+        nc.sync.dma_start(out_rows[:, 0:2, :], res0[:])
+        res1 = keep.tile([P, 2, V], F32, name="res1")
+        nc.vector.tensor_tensor(res1[:], num[:, 2:4, :], rec_s[:], MULT)
+        nc.sync.dma_start(out_rows[:, 2:4, :], res1[:])

@@ -35,6 +35,7 @@ PARTS = 2
 PART_BLOCKS = BLOCKS // PARTS
 HALF_ROW = P - 2
 VAL_ROW = P - 1
+SCALAR_CLEARS = 256
 BANKS = 8
 FLOPS = 2 * K * H * S + 2 * H * S * U
 
@@ -59,8 +60,13 @@ def tile_picked_ynw_avg_p_kernel(
         w_raw1b = after_cast.tile([P, PACK, H // 2], F32, name="w_raw1b", offset=0, align_bytes=64)
         w_pieces = [[(w_raw0, 0, H)], [(w_raw1a, 0, H // 2), (w_raw1b, H // 2, H)]]
 
-        nc.vector.memset(xs_win[:].bitcast(I32), 0)
-        nc.vector.memset(hv_win[0:HALF_ROW, :], 0.0)
+        nc.vector.memset(es_win[:].bitcast(I32), 0)
+        zero = keep.tile([P, 1], F32, name="zero")
+        nc.gpsimd.memset(zero[:], 0.0)
+        nc.vector.memset(hv_win[0:HALF_ROW, 0 : W // 2], 0.0)
+        nc.gpsimd.memset(hv_win[0:HALF_ROW, W // 2 : W - SCALAR_CLEARS], 0.0)
+        nc.gpsimd.memset(xs_win[:].bitcast(I32), 0)
+        nc.scalar.copy(hv_win[0:HALF_ROW, W - SCALAR_CLEARS : W], zero[0:HALF_ROW, :].to_broadcast([HALF_ROW, SCALAR_CLEARS]))
 
         xw_win = [keep.tile([P, T], I32, name="xw_win%d" % o, align_bytes=64) for o in range(PASSES)]
         ew_win = keep.tile([P, W], I32, name="ew_win")
@@ -73,18 +79,21 @@ def tile_picked_ynw_avg_p_kernel(
         nc.sync.dma_start(ex_list[:], ex)
         nc.scalar.dma_start(hv_win[HALF_ROW : HALF_ROW + 1, :], half[0:1, :])
         nc.sync.dma_start(hv_win[VAL_ROW : VAL_ROW + 1, :], val[0:1, :])
+        for j in range(PACK):
+            nc.sync.dma_start(w_raw0[:, j, :], w1[j:PASS_ROWS:PACK, :])
         for q in range(QUADRANTS):
-            scale_rows = e_scales[0:1, 4 * q : 4 * q + 4, :].bitcast(I32).broadcast_to([QUADRANT // 4, 4, W // 4])
-            nc.sync.dma_start(es_win[QUADRANT * q : QUADRANT * (q + 1), :].bitcast(I32), scale_rows)
-        load_w(0, 0)
+            nc.sync.dma_start(
+                es_win[QUADRANT * q : QUADRANT * q + 4, :].bitcast(I32),
+                e_scales[0, 4 * q : 4 * q + 4, :].bitcast(I32),
+            )
         load_w(1, 0)
-        nc.sync.dma_start(offs_list[:], offs)
+        nc.sync.dma_start(xw_win[0][:], x_words[0].rearrange("p n j -> p (n j)").bitcast(I32))
         for q in range(QUADRANTS):
             nc.sync.dma_start(
                 xs_win[QUADRANT * q : QUADRANT * q + 4 * PASSES, :].bitcast(I32),
                 x_scales[:, 4 * q : 4 * q + 4, :].bitcast(I32),
             )
-        nc.sync.dma_start(xw_win[0][:], x_words[0].rearrange("p n j -> p (n j)").bitcast(I32))
+        nc.sync.dma_start(offs_list[:], offs)
         load_w(1, 1)
         nc.sync.dma_start(xw_win[1][:], x_words[1].rearrange("p n j -> p (n j)").bitcast(I32))
         nc.sync.dma_start(ew_win[:], e_words[0].rearrange("p n j -> p (n j)").bitcast(I32))
@@ -105,17 +114,16 @@ def tile_picked_ynw_avg_p_kernel(
                     w_bf[:].rearrange("p (t m j) -> p m j t", t=PACK, j=PACK)[:, first // PACK : end // PACK],
                     raw[:].rearrange("p j (m t) -> p m j t", t=PACK),
                 )
-            codes = keep.tile([P, H], U32, name="w_codes%d" % o, align_bytes=64)
+            codes = keep.tile([P, H], U32, name="w_codes%d" % o, tag=("xw_win0", "w_codes1")[o], align_bytes=64)
             scales = keep.tile([P, H], U8, name="w_scales%d" % o, align_bytes=64)
             nc.vector.quantize_mx(codes[:].bitcast(FP8X4), scales[:], w_bf[:])
             return codes, scales
 
-        w_mx = [quantize_w(0)]
-        xs = keep.tile([P, S], U8, name="xs", align_bytes=64)
-        nc.vector.tensor_copy(xs[:], xs_win[:].indirect(offs_list[:]))
         xw0 = keep.tile([P, S], U32, name="xw0", align_bytes=64)
         nc.vector.tensor_copy(xw0[:], xw_win[0][:].bitcast(U32).indirect(offs_list[:]))
-        w_mx.append(quantize_w(1))
+        xs = keep.tile([P, S], U8, name="xs", align_bytes=64)
+        nc.vector.tensor_copy(xs[:], xs_win[:].indirect(offs_list[:]))
+        w_mx = [quantize_w(o) for o in range(PASSES)]
         xw = [[xw0[:, P * b : P * (b + 1)] for b in range(BLOCKS)], []]
         for u in range(2):
             words = after_cast.tile([P, S // 2], U32, name="xw1_%d" % u, offset=2 * S * u, align_bytes=64)

@@ -36,7 +36,6 @@ PART_BLOCKS = BLOCKS // PARTS
 HALF_ROW = P - 2
 VAL_ROW = P - 1
 SCALAR_CLEARS = 256
-BANKS = 8
 FLOPS = 2 * K * H * S + 2 * H * S * U
 
 
@@ -48,7 +47,8 @@ def tile_picked_ynw_avg_p_kernel(
         keep = ctx.enter_context(tc.tile_pool(name="keep", bufs=1))
         late = ctx.enter_context(tc.tile_pool(name="late", bufs=1))
         after_cast = ctx.enter_context(tc.tile_pool(name="after_cast", bufs=1))
-        banks = ctx.enter_context(tc.psum_pool(name="banks", bufs=BANKS))
+        banks = ctx.enter_context(tc.psum_pool(name="banks", bufs=1))
+        sums = ctx.enter_context(tc.psum_pool(name="sums", bufs=BLOCKS))
 
         ex_list = keep.tile([P, U // 16], U16, name="ex_list")
         offs_list = keep.tile([P, S // 16], U16, name="offs_list")
@@ -135,7 +135,7 @@ def tile_picked_ynw_avg_p_kernel(
         neg_half = hv_col[:, 0, :]
         val_col = hv_col[:, 1, :]
         for a in range(D // PACK):
-            hv_ps = banks.tile([P, PACK, P], F32, name="hv_ps", tag="bank")
+            hv_ps = sums.tile([P, PACK, P], F32, name="hv_ps", tag="sum")
             for c in range(PACK):
                 nc.tensor.transpose(hv_ps[:, c, :], hv_ex[:, PACK * a + c : U : D], ident[:])
             nc.scalar.mul(neg_half[:, PACK * a : PACK * (a + 1)], hv_ps[:, :, HALF_ROW], -1.0)
@@ -148,7 +148,7 @@ def tile_picked_ynw_avg_p_kernel(
         h_bf = late.tile([P, S, PACK], BF16, name="h_bf", offset=0, align_bytes=64)
         h_codes = keep.tile([P, S], U32, name="h_codes", align_bytes=64)
         h_scales = keep.tile([P, S], U8, name="h_scales", align_bytes=64)
-        h_ps = [banks.tile([P, PACK, P], F32, name="h_ps%d" % b, tag="bank") for b in range(BLOCKS)]
+        h_ps = [banks.tile([P, PACK, P], F32, name="h_ps%d" % b, tag="bank%d" % b) for b in range(BLOCKS)]
         for o in range(PASSES):
             w_codes, w_scales = w_mx[o]
             for b in range(BLOCKS):
@@ -179,7 +179,11 @@ def tile_picked_ynw_avg_p_kernel(
         e_codes0 = keep.tile([P, U // 2], U32, name="e_codes0", align_bytes=64)
         e_bytes0 = keep.tile([P, U // 2], U8, name="e_bytes0", tag="w_bf1", align_bytes=64)
         deal(0, e_codes0, e_bytes0)
-        nc.vector.quantize_mx(h_codes[:].bitcast(FP8X4), h_scales[:], h_bf[:].rearrange("p n t -> p (n t)"))
+        halves = [slice(0, S // 2), slice(S // 2, S)]
+        for part in halves:
+            nc.vector.quantize_mx(
+                h_codes[:, part].bitcast(FP8X4), h_scales[:, part], h_bf[:, part, :].rearrange("p n t -> p (n t)")
+            )
         e_codes1 = late.tile([P, U // 2], U32, name="e_codes1", offset=0, align_bytes=64)
         e_bytes1 = late.tile([P, U // 2], U8, name="e_bytes1", offset=2 * U, align_bytes=64)
         deal(1, e_codes1, e_bytes1)
@@ -187,19 +191,26 @@ def tile_picked_ynw_avg_p_kernel(
         e_bytes = [e_bytes0, e_bytes1]
 
         ee = [keep.tile([P, S], F32, name="ee%d" % d) for d in range(D)]
-        for d in range(D):
-            y_ps = banks.tile([P, S], F32, name="y_ps", tag="bank")
+
+        def weigh(d, y_ps, part):
             member = slice(V * (d % 4), V * (d % 4 + 1))
             nc.tensor.matmul_mx(
-                y_ps[:],
+                y_ps,
                 lhsT=e_codes[d // 4][:, member].bitcast(FP8X4),
                 lhsT_scale=e_bytes[d // 4][:, member],
-                rhs=h_codes[:].bitcast(FP8X4),
-                rhs_scale=h_scales[:],
+                rhs=h_codes[:, part].bitcast(FP8X4),
+                rhs_scale=h_scales[:, part],
                 start=True,
                 stop=True,
             )
-            nc.scalar.activation(ee[d][:], y_ps[:], EXP, bias=neg_half[:, d : d + 1], scale=0.5)
+            nc.scalar.activation(ee[d][:, part], y_ps, EXP, bias=neg_half[:, d : d + 1], scale=0.5)
+
+        y_first = sums.tile([P, S // 2], F32, name="y_first", tag="sum")
+        weigh(0, y_first[:], halves[0])
+        for d in range(D):
+            y_ps = banks.tile([P, S], F32, name="y_ps", tag="bank%d" % (d % BLOCKS))
+            part = halves[1] if d == 0 else slice(0, S)
+            weigh(d, y_ps[:, part], part)
 
         table_warm = keep.tile([P, 1], F32, name="table_warm")
         nc.scalar.activation(table_warm[:], ee[D - 1][:, 0:1], RSQRT)
@@ -217,19 +228,18 @@ def tile_picked_ynw_avg_p_kernel(
         def add_turned(dst, term, b, start, stop):
             nc.tensor.matmul(dst, term[:, P * b : P * (b + 1)], ident[:], is_transpose=True, start=start, stop=stop)
 
-        den_v = banks.tile([P, V], F32, name="den_v", tag="bank")
-        den_s = banks.tile([P, BLOCKS - 1, V], F32, name="den_s", tag="bank")
-        num = banks.tile([P, BLOCKS, V], F32, name="num", tag="bank")
+        den_v = sums.tile([P, V], F32, name="den_v", tag="sum")
+        den_s = sums.tile([P, BLOCKS - 1, V], F32, name="den_s", tag="sum")
+        num = banks.tile([P, BLOCKS, V], F32, name="num", tag="bank%d" % (BLOCKS - 1))
         den_terms = [first_two] + ee[2:]
-        num_terms = {4: acc[1], 5: acc[0], 6: last}
         for i, term in enumerate(den_terms):
             final = i == len(den_terms) - 1
             add_turned(den_v[:], term, 0, i == 0, final)
             for b in range(1, BLOCKS):
                 add_turned(den_s[:, b - 1, :], term, b, i == 0 and b == 1, final and b == BLOCKS - 1)
-            if i in num_terms:
-                for b in range(BLOCKS):
-                    add_turned(num[:, b, :], num_terms[i], b, i == 4 and b == 0, final and b == BLOCKS - 1)
+        for i, term in enumerate([acc[1], acc[0], last]):
+            for b in range(BLOCKS):
+                add_turned(num[:, b, :], term, b, i == 0 and b == 0, i == 2 and b == BLOCKS - 1)
 
         out_rows = out.rearrange("(b p) v -> p b v", p=P)
         rec_v = keep.tile([P, V], F32, name="rec_v")

@@ -54,7 +54,7 @@ def tile_picked_ynw_avg_p_kernel(
         offs_list = keep.tile([P, S // 16], U16, name="offs_list")
         hv_win = keep.tile([P, W], F32, name="hv_win")
         es_win = keep.tile([P, W], U8, name="es_win", align_bytes=64)
-        xs_win = keep.tile([P, T], U8, name="xs_win")
+        xs_win = keep.tile([P, T], U8, name="xs_win", align_bytes=64)
         w_raw0 = keep.tile([P, PACK, H], F32, name="w_raw0")
         w_raw1a = keep.tile([P, PACK, H // 2], F32, name="w_raw1a")
         w_raw1b = after_cast.tile([P, PACK, H // 2], F32, name="w_raw1b", offset=0, align_bytes=64)
@@ -114,22 +114,26 @@ def tile_picked_ynw_avg_p_kernel(
                     w_bf[:].rearrange("p (t m j) -> p m j t", t=PACK, j=PACK)[:, first // PACK : end // PACK],
                     raw[:].rearrange("p j (m t) -> p m j t", t=PACK),
                 )
-            codes = keep.tile([P, H], U32, name="w_codes%d" % o, tag=("xw_win0", "w_codes1")[o], align_bytes=64)
+            codes = keep.tile([P, H], U32, name="w_codes%d" % o, tag=("xs_win", "w_codes1")[o], align_bytes=64)
             scales = keep.tile([P, H], U8, name="w_scales%d" % o, align_bytes=64)
             nc.vector.quantize_mx(codes[:].bitcast(FP8X4), scales[:], w_bf[:])
             return codes, scales
 
-        xw0 = keep.tile([P, S], U32, name="xw0", align_bytes=64)
-        nc.vector.tensor_copy(xw0[:], xw_win[0][:].bitcast(U32).indirect(offs_list[:]))
         xs = keep.tile([P, S], U8, name="xs", align_bytes=64)
         nc.vector.tensor_copy(xs[:], xs_win[:].indirect(offs_list[:]))
-        w_mx = [quantize_w(o) for o in range(PASSES)]
-        xw = [[xw0[:, P * b : P * (b + 1)] for b in range(BLOCKS)], []]
-        for u in range(2):
-            words = after_cast.tile([P, S // 2], U32, name="xw1_%d" % u, offset=2 * S * u, align_bytes=64)
+        xw = [[], []]
+
+        def gather_x(o, u, words):
             entries = offs_list[:, u * S // 32 : (u + 1) * S // 32]
-            nc.vector.tensor_copy(words[:], xw_win[1][:].bitcast(U32).indirect(entries))
-            xw[1].extend(words[:, P * b : P * (b + 1)] for b in range(BLOCKS // 2))
+            nc.vector.tensor_copy(words[:], xw_win[o][:].bitcast(U32).indirect(entries))
+            xw[o].extend(words[:, P * b : P * (b + 1)] for b in range(BLOCKS // 2))
+
+        gather_x(0, 0, keep.tile([P, S // 2], U32, name="xw0_0", align_bytes=64))
+        w_mx = [quantize_w(0)]
+        gather_x(0, 1, after_cast.tile([P, S // 2], U32, name="xw0_1", offset=6 * S, align_bytes=64))
+        w_mx.append(quantize_w(1))
+        for u in range(2):
+            gather_x(1, u, after_cast.tile([P, S // 2], U32, name="xw1_%d" % u, offset=2 * S * u, align_bytes=64))
 
         hv_col = after_cast.tile([P, 2, D], F32, name="hv_col", offset=4 * S)
         neg_half = hv_col[:, 0, :]
@@ -166,38 +170,43 @@ def tile_picked_ynw_avg_p_kernel(
                 if o == PASSES - 1:
                     nc.scalar.copy(h_bf[:, queries, :], h_ps[b][:].rearrange("p t n -> p n t"))
 
-        def deal(a, codes, scale_bytes):
-            nc.vector.tensor_copy(
-                scale_bytes[:].rearrange("p (c v) -> p v c", c=4),
-                es_ex[:].rearrange("p (v a c) -> p a v c", a=2, c=4)[:, a],
-            )
-            nc.vector.tensor_copy(
-                codes[:].rearrange("p (c vq vl) -> p vq c vl", c=4, vl=4),
-                ew_ex[:].rearrange("p (vq vl a c) -> p a vq c vl", a=2, c=4, vl=4)[:, a],
-            )
+        e_codes = []
+        e_bytes = []
 
-        e_codes0 = keep.tile([P, U // 2], U32, name="e_codes0", align_bytes=64)
-        e_bytes0 = keep.tile([P, U // 2], U8, name="e_bytes0", tag="w_bf1", align_bytes=64)
-        deal(0, e_codes0, e_bytes0)
+        def deal(first, count, codes, scale_bytes):
+            members = slice(first, first + count)
+            nc.vector.tensor_copy(
+                scale_bytes[:].rearrange("p (c v) -> p v c", c=count),
+                es_ex[:].rearrange("p (v d) -> p v d", d=D)[:, :, members],
+            )
+            nc.vector.tensor_copy(
+                codes[:].rearrange("p (c vq vl) -> p vq c vl", c=count, vl=4),
+                ew_ex[:].rearrange("p (vq vl d) -> p vq d vl", d=D, vl=4)[:, :, members, :],
+            )
+            e_codes.extend(codes[:, V * c : V * (c + 1)] for c in range(count))
+            e_bytes.extend(scale_bytes[:, V * c : V * (c + 1)] for c in range(count))
+
+        codes01 = keep.tile([P, 2 * V], U32, name="codes01", align_bytes=64)
+        bytes01 = keep.tile([P, 2 * V], U8, name="bytes01", tag="w_bf1", align_bytes=64)
+        deal(0, 2, codes01, bytes01)
         halves = [slice(0, S // 2), slice(S // 2, S)]
         for part in halves:
             nc.vector.quantize_mx(
                 h_codes[:, part].bitcast(FP8X4), h_scales[:, part], h_bf[:, part, :].rearrange("p n t -> p (n t)")
             )
-        e_codes1 = late.tile([P, U // 2], U32, name="e_codes1", offset=0, align_bytes=64)
-        e_bytes1 = late.tile([P, U // 2], U8, name="e_bytes1", offset=2 * U, align_bytes=64)
-        deal(1, e_codes1, e_bytes1)
-        e_codes = [e_codes0, e_codes1]
-        e_bytes = [e_bytes0, e_bytes1]
+        for first, count in ((2, 2), (4, 4)):
+            offset = 5 * V * (first - 2)
+            codes = late.tile([P, count * V], U32, name="codes%d" % first, offset=offset, align_bytes=64)
+            scale_bytes = late.tile([P, count * V], U8, name="bytes%d" % first, offset=offset + 4 * count * V, align_bytes=64)
+            deal(first, count, codes, scale_bytes)
 
         ee = [keep.tile([P, S], F32, name="ee%d" % d) for d in range(D)]
 
         def weigh(d, y_ps, part):
-            member = slice(V * (d % 4), V * (d % 4 + 1))
             nc.tensor.matmul_mx(
                 y_ps,
-                lhsT=e_codes[d // 4][:, member].bitcast(FP8X4),
-                lhsT_scale=e_bytes[d // 4][:, member],
+                lhsT=e_codes[d].bitcast(FP8X4),
+                lhsT_scale=e_bytes[d],
                 rhs=h_codes[:, part].bitcast(FP8X4),
                 rhs_scale=h_scales[:, part],
                 start=True,
@@ -222,8 +231,10 @@ def tile_picked_ynw_avg_p_kernel(
         nc.vector.tensor_tensor(first_two[:], ee[0][:], ee[1][:], ADD)
         for d in range(2, D - 1):
             nc.vector.scalar_tensor_tensor(acc[d % 2][:], ee[d][:], val_col[:, d : d + 1], acc[d % 2][:], MULT, ADD)
-        last = keep.tile([P, S], F32, name="last")
-        nc.vector.tensor_scalar(last[:], ee[D - 1][:], val_col[:, D - 1 : D], None, MULT)
+        for part in halves:
+            nc.vector.scalar_tensor_tensor(
+                acc[1][:, part], ee[D - 1][:, part], val_col[:, D - 1 : D], acc[1][:, part], MULT, ADD
+            )
 
         def add_turned(dst, term, b, start, stop):
             nc.tensor.matmul(dst, term[:, P * b : P * (b + 1)], ident[:], is_transpose=True, start=start, stop=stop)
@@ -237,23 +248,24 @@ def tile_picked_ynw_avg_p_kernel(
             add_turned(den_v[:], term, 0, i == 0, final)
             for b in range(1, BLOCKS):
                 add_turned(den_s[:, b - 1, :], term, b, i == 0 and b == 1, final and b == BLOCKS - 1)
-        for i, term in enumerate([acc[1], acc[0], last]):
+        for i in range(2):
             for b in range(BLOCKS):
-                add_turned(num[:, b, :], term, b, i == 0 and b == 0, i == 2 and b == BLOCKS - 1)
+                add_turned(num[:, b, :], acc[i], b, i == 0 and b == 0, i == 1 and b == BLOCKS - 1)
 
         out_rows = out.rearrange("(b p) v -> p b v", p=P)
         rec_v = keep.tile([P, V], F32, name="rec_v")
         nc.vector.reciprocal(rec_v[:], den_v[:])
         root = keep.tile([P, BLOCKS - 1, V], F32, name="root")
         nc.scalar.activation(root[:], den_s[:], RSQRT)
-        rec_s = keep.tile([P, 2, V], F32, name="rec_s")
-        nc.scalar.activation(rec_s[:], root[:, 1:3, :], SQUARE)
-        once = keep.tile([P, V], F32, name="once")
-        nc.vector.tensor_tensor(once[:], num[:, 1, :], root[:, 0, :], MULT)
-        res0 = keep.tile([P, 2, V], F32, name="res0")
-        nc.vector.tensor_tensor(res0[:, 0, :], num[:, 0, :], rec_v[:], MULT)
-        nc.vector.tensor_tensor(res0[:, 1, :], once[:], root[:, 0, :], MULT)
-        nc.sync.dma_start(out_rows[:, 0:2, :], res0[:])
-        res1 = keep.tile([P, 2, V], F32, name="res1")
-        nc.vector.tensor_tensor(res1[:], num[:, 2:4, :], rec_s[:], MULT)
-        nc.sync.dma_start(out_rows[:, 2:4, :], res1[:])
+        rec_s = keep.tile([P, BLOCKS - 1, V], F32, name="rec_s")
+        nc.scalar.activation(rec_s[:, 0, :], root[:, 0, :], SQUARE)
+        nc.scalar.activation(rec_s[:, 1:3, :], root[:, 1:3, :], SQUARE)
+
+        def finish(first, end, factor):
+            res = keep.tile([P, end - first, V], F32, name="res%d" % first)
+            nc.vector.tensor_tensor(res[:], num[:, first:end, :], factor, MULT)
+            nc.sync.dma_start(out_rows[:, first:end, :], res[:])
+
+        finish(0, 1, rec_v[:].unsqueeze(1))
+        finish(1, 2, rec_s[:, 0:1, :])
+        finish(2, 4, rec_s[:, 1:3, :])

@@ -60,7 +60,8 @@ def tile_picked_ynw_avg_p_kernel(
         w_raw1b = after_cast.tile([P, PACK, H // 2], F32, name="w_raw1b", offset=0, align_bytes=64)
         w_pieces = [[(w_raw0, 0, H)], [(w_raw1a, 0, H // 2), (w_raw1b, H // 2, H)]]
 
-        nc.vector.memset(es_win[:].bitcast(I32), 0)
+        nc.vector.memset(es_win[:, 0 : W // 2].bitcast(I32), 0)
+        nc.gpsimd.memset(es_win[:, W // 2 : W].bitcast(I32), 0)
         zero = keep.tile([P, 1], F32, name="zero")
         nc.gpsimd.memset(zero[:], 0.0)
         nc.vector.memset(hv_win[0:HALF_ROW, 0 : W // 2], 0.0)
@@ -79,8 +80,7 @@ def tile_picked_ynw_avg_p_kernel(
         nc.sync.dma_start(ex_list[:], ex)
         nc.scalar.dma_start(hv_win[HALF_ROW : HALF_ROW + 1, :], half[0:1, :])
         nc.sync.dma_start(hv_win[VAL_ROW : VAL_ROW + 1, :], val[0:1, :])
-        for j in range(PACK):
-            nc.sync.dma_start(w_raw0[:, j, :], w1[j:PASS_ROWS:PACK, :])
+        load_w(0, 0)
         for q in range(QUADRANTS):
             nc.sync.dma_start(
                 es_win[QUADRANT * q : QUADRANT * q + 4, :].bitcast(I32),

@@ -35,6 +35,7 @@ PARTS = 2
 PART_BLOCKS = BLOCKS // PARTS
 HALF_ROW = P - 2
 VAL_ROW = P - 1
+E_PLANE = 8
 SCALAR_CLEARS = 256
 FLOPS = 2 * K * H * S + 2 * H * S * U
 
@@ -83,7 +84,7 @@ def tile_picked_ynw_avg_p_kernel(
         load_w(0, 0)
         for q in range(QUADRANTS):
             nc.sync.dma_start(
-                es_win[QUADRANT * q : QUADRANT * q + 4, :].bitcast(I32),
+                es_win[QUADRANT * q + E_PLANE : QUADRANT * q + E_PLANE + 4, :].bitcast(I32),
                 e_scales[0, 4 * q : 4 * q + 4, :].bitcast(I32),
             )
         load_w(1, 0)
@@ -184,7 +185,7 @@ def tile_picked_ynw_avg_p_kernel(
                 ew_ex[:].rearrange("p (vq vl d) -> p vq d vl", d=D, vl=4)[:, :, members, :],
             )
             e_codes.extend(codes[:, V * c : V * (c + 1)] for c in range(count))
-            e_bytes.extend(scale_bytes[:, V * c : V * (c + 1)] for c in range(count))
+            e_bytes.extend(scale_bytes[E_PLANE:P, V * c : V * (c + 1)] for c in range(count))
 
         codes01 = keep.tile([P, 2 * V], U32, name="codes01", align_bytes=64)
         bytes01 = keep.tile([P, 2 * V], U8, name="bytes01", tag="w_bf1", align_bytes=64)
@@ -222,7 +223,7 @@ def tile_picked_ynw_avg_p_kernel(
             weigh(d, y_ps[:, part], part)
 
         table_warm = keep.tile([P, 1], F32, name="table_warm")
-        nc.scalar.activation(table_warm[:], ee[D - 1][:, 0:1], RSQRT)
+        nc.scalar.activation(table_warm[:], ee[D - 2][:, 0:1], RSQRT)
 
         acc = [keep.tile([P, S], F32, name="acc%d" % i) for i in range(2)]
         for d in range(2):
@@ -241,31 +242,34 @@ def tile_picked_ynw_avg_p_kernel(
 
         den_v = sums.tile([P, V], F32, name="den_v", tag="sum")
         den_s = sums.tile([P, BLOCKS - 1, V], F32, name="den_s", tag="sum")
-        num = banks.tile([P, BLOCKS, V], F32, name="num", tag="bank%d" % (BLOCKS - 1))
+        num = [banks.tile([P, 2, V], F32, name="num%d" % g, tag="bank%d" % (BLOCKS - 1 - g)) for g in range(2)]
         den_terms = [first_two] + ee[2:]
         for i, term in enumerate(den_terms):
             final = i == len(den_terms) - 1
             add_turned(den_v[:], term, 0, i == 0, final)
             for b in range(1, BLOCKS):
                 add_turned(den_s[:, b - 1, :], term, b, i == 0 and b == 1, final and b == BLOCKS - 1)
-        for i in range(2):
-            for b in range(BLOCKS):
-                add_turned(num[:, b, :], acc[i], b, i == 0 and b == 0, i == 1 and b == BLOCKS - 1)
+        for g in range(2):
+            for i in range(2):
+                for b in range(2):
+                    add_turned(num[g][:, b, :], acc[i], 2 * g + b, i == 0 and b == 0, i == 1 and b == 1)
 
         out_rows = out.rearrange("(b p) v -> p b v", p=P)
         rec_v = keep.tile([P, V], F32, name="rec_v")
         nc.vector.reciprocal(rec_v[:], den_v[:])
         root = keep.tile([P, BLOCKS - 1, V], F32, name="root")
-        nc.scalar.activation(root[:], den_s[:], RSQRT)
-        rec_s = keep.tile([P, BLOCKS - 1, V], F32, name="rec_s")
-        nc.scalar.activation(rec_s[:, 0, :], root[:, 0, :], SQUARE)
-        nc.scalar.activation(rec_s[:, 1:3, :], root[:, 1:3, :], SQUARE)
+        nc.scalar.activation(root[:, 0, :], den_s[:, 0, :], RSQRT)
+        nc.scalar.activation(root[:, 1:3, :], den_s[:, 1:3, :], RSQRT)
+        rec_s = keep.tile([P, 2, V], F32, name="rec_s")
+        nc.scalar.activation(rec_s[:], root[:, 1:3, :], SQUARE)
 
-        def finish(first, end, factor):
+        def finish(first, end, numerator, factor):
             res = keep.tile([P, end - first, V], F32, name="res%d" % first)
-            nc.vector.tensor_tensor(res[:], num[:, first:end, :], factor, MULT)
+            nc.vector.tensor_tensor(res[:], numerator, factor, MULT)
             nc.sync.dma_start(out_rows[:, first:end, :], res[:])
 
-        finish(0, 1, rec_v[:].unsqueeze(1))
-        finish(1, 2, rec_s[:, 0:1, :])
-        finish(2, 4, rec_s[:, 1:3, :])
+        once = keep.tile([P, 1, V], F32, name="once")
+        nc.vector.tensor_tensor(once[:], num[0][:, 1:2, :], root[:, 0:1, :], MULT)
+        finish(0, 1, num[0][:, 0:1, :], rec_v[:].unsqueeze(1))
+        finish(1, 2, once[:], root[:, 0:1, :])
+        finish(2, 4, num[1][:], rec_s[:])

@@ -36,7 +36,7 @@ PART_BLOCKS = BLOCKS // PARTS
 HALF_ROW = P - 2
 VAL_ROW = P - 1
 E_PLANE = 8
-SCALAR_CLEARS = 256
+FIRST_GROUPS = 96
 FLOPS = 2 * K * H * S + 2 * H * S * U
 
 
@@ -47,75 +47,69 @@ def tile_picked_ynw_avg_p_kernel(
     with ExitStack() as ctx:
         keep = ctx.enter_context(tc.tile_pool(name="keep", bufs=1))
         late = ctx.enter_context(tc.tile_pool(name="late", bufs=1))
-        after_cast = ctx.enter_context(tc.tile_pool(name="after_cast", bufs=1))
+        e_side = ctx.enter_context(tc.tile_pool(name="e_side", bufs=1))
         banks = ctx.enter_context(tc.psum_pool(name="banks", bufs=1))
         sums = ctx.enter_context(tc.psum_pool(name="sums", bufs=BLOCKS))
 
         ex_list = keep.tile([P, U // 16], U16, name="ex_list")
         offs_list = keep.tile([P, S // 16], U16, name="offs_list")
         hv_win = keep.tile([P, W], F32, name="hv_win")
-        es_win = keep.tile([P, W], U8, name="es_win", align_bytes=64)
+        es_win = e_side.tile([P, W], U8, name="es_win", offset=0, align_bytes=64)
+        es_planes = keep.tile([P, U], U8, name="es_planes")
         xs_win = keep.tile([P, T], U8, name="xs_win", align_bytes=64)
-        w_raw0 = keep.tile([P, PACK, H], F32, name="w_raw0")
-        w_raw1a = keep.tile([P, PACK, H // 2], F32, name="w_raw1a")
-        w_raw1b = after_cast.tile([P, PACK, H // 2], F32, name="w_raw1b", offset=0, align_bytes=64)
-        w_pieces = [[(w_raw0, 0, H)], [(w_raw1a, 0, H // 2), (w_raw1b, H // 2, H)]]
+        w_raw = [keep.tile([P, PACK, H], F32, name="w_raw%d" % o) for o in range(PASSES)]
+        xw_win = [keep.tile([P, T], I32, name="xw_win%d" % o, align_bytes=64) for o in range(PASSES)]
 
-        nc.vector.memset(es_win[:, 0 : W // 2].bitcast(I32), 0)
-        nc.gpsimd.memset(es_win[:, W // 2 : W].bitcast(I32), 0)
+        nc.vector.memset(xs_win[:].bitcast(I32), 0)
         zero = keep.tile([P, 1], F32, name="zero")
         nc.gpsimd.memset(zero[:], 0.0)
-        nc.vector.memset(hv_win[0:HALF_ROW, 0 : W // 2], 0.0)
-        nc.gpsimd.memset(hv_win[0:HALF_ROW, W // 2 : W - SCALAR_CLEARS], 0.0)
-        nc.gpsimd.memset(xs_win[:].bitcast(I32), 0)
-        nc.scalar.copy(hv_win[0:HALF_ROW, W - SCALAR_CLEARS : W], zero[0:HALF_ROW, :].to_broadcast([HALF_ROW, SCALAR_CLEARS]))
+        nc.vector.memset(es_win[0:16, :].bitcast(I32), 0)
+        nc.gpsimd.memset(es_win[32:64, :].bitcast(I32), 0)
+        nc.gpsimd.memset(es_win[64:P, :].bitcast(I32), 0)
+        nc.scalar.copy(hv_win[0:HALF_ROW, :], zero[0:HALF_ROW, :].to_broadcast([HALF_ROW, W]))
+        nc.vector.memset(es_planes[:].bitcast(I32), 0)
 
-        xw_win = [keep.tile([P, T], I32, name="xw_win%d" % o, align_bytes=64) for o in range(PASSES)]
-        ew_win = keep.tile([P, W], I32, name="ew_win")
-
-        def load_w(o, piece):
-            raw, first, end = w_pieces[o][piece]
-            rows = w1[o * PASS_ROWS : (o + 1) * PASS_ROWS, first:end]
-            nc.sync.dma_start(raw[:], rows.rearrange("(p j) c -> p j c", j=PACK))
+        def load_w(o):
+            rows = w1[o * PASS_ROWS : (o + 1) * PASS_ROWS, :]
+            nc.sync.dma_start(w_raw[o][:], rows.rearrange("(p j) c -> p j c", j=PACK))
 
         nc.sync.dma_start(ex_list[:], ex)
+        nc.sync.dma_start(es_win[16:32, :].bitcast(I32), e_scales[0].bitcast(I32))
         nc.scalar.dma_start(hv_win[HALF_ROW : HALF_ROW + 1, :], half[0:1, :])
         nc.sync.dma_start(hv_win[VAL_ROW : VAL_ROW + 1, :], val[0:1, :])
-        load_w(0, 0)
-        for q in range(QUADRANTS):
-            nc.sync.dma_start(
-                es_win[QUADRANT * q + E_PLANE : QUADRANT * q + E_PLANE + 4, :].bitcast(I32),
-                e_scales[0, 4 * q : 4 * q + 4, :].bitcast(I32),
-            )
-        load_w(1, 0)
-        nc.sync.dma_start(xw_win[0][:], x_words[0].rearrange("p n j -> p (n j)").bitcast(I32))
+        load_w(0)
         for q in range(QUADRANTS):
             nc.sync.dma_start(
                 xs_win[QUADRANT * q : QUADRANT * q + 4 * PASSES, :].bitcast(I32),
                 x_scales[:, 4 * q : 4 * q + 4, :].bitcast(I32),
             )
         nc.sync.dma_start(offs_list[:], offs)
-        load_w(1, 1)
-        nc.sync.dma_start(xw_win[1][:], x_words[1].rearrange("p n j -> p (n j)").bitcast(I32))
-        nc.sync.dma_start(ew_win[:], e_words[0].rearrange("p n j -> p (n j)").bitcast(I32))
+        load_w(1)
+        for o in range(PASSES):
+            nc.sync.dma_start(xw_win[o][:], x_words[o].rearrange("p n j -> p (n j)").bitcast(I32))
 
         ident = keep.tile([P, P], F32, name="ident")
         make_identity(nc, ident[:])
 
-        hv_ex = keep.tile([P, U], F32, name="hv_ex")
-        nc.vector.tensor_copy(hv_ex[:], hv_win[:].indirect(ex_list[:]))
-
         es_ex = keep.tile([P, U], U8, name="es_ex")
         nc.vector.tensor_copy(es_ex[:], es_win[:].indirect(ex_list[:]))
+        for q in range(QUADRANTS):
+            first = QUADRANT * q + E_PLANE
+            nc.sync.dma_start(
+                es_planes[first : first + 4, :].bitcast(I32), es_ex[16 + 4 * q : 20 + 4 * q, :].bitcast(I32)
+            )
+        hv_ex = keep.tile([P, U], F32, name="hv_ex")
+        nc.vector.tensor_copy(hv_ex[:], hv_win[:].indirect(ex_list[:]))
+        ew_win = e_side.tile([P, W], I32, name="ew_win", offset=0, align_bytes=64)
+        nc.sync.dma_start(ew_win[:], e_words[0].rearrange("p n j -> p (n j)").bitcast(I32))
 
         def quantize_w(o):
             w_bf = keep.tile([P, PACK * H], BF16, name="w_bf%d" % o, align_bytes=64)
-            for raw, first, end in w_pieces[o]:
-                nc.scalar.copy(
-                    w_bf[:].rearrange("p (t m j) -> p m j t", t=PACK, j=PACK)[:, first // PACK : end // PACK],
-                    raw[:].rearrange("p j (m t) -> p m j t", t=PACK),
-                )
-            codes = keep.tile([P, H], U32, name="w_codes%d" % o, tag=("xs_win", "w_codes1")[o], align_bytes=64)
+            nc.scalar.copy(
+                w_bf[:].rearrange("p (t m j) -> p m j t", t=PACK, j=PACK),
+                w_raw[o][:].rearrange("p j (m t) -> p m j t", t=PACK),
+            )
+            codes = keep.tile([P, H], U32, name="w_codes%d" % o, align_bytes=64)
             scales = keep.tile([P, H], U8, name="w_scales%d" % o, align_bytes=64)
             nc.vector.quantize_mx(codes[:].bitcast(FP8X4), scales[:], w_bf[:])
             return codes, scales
@@ -123,20 +117,16 @@ def tile_picked_ynw_avg_p_kernel(
         xs = keep.tile([P, S], U8, name="xs", align_bytes=64)
         nc.vector.tensor_copy(xs[:], xs_win[:].indirect(offs_list[:]))
         xw = [[], []]
+        w_mx = []
+        for o in range(PASSES):
+            w_mx.append(quantize_w(o))
+            for u in range(2):
+                words = keep.tile([P, S // 2], U32, name="xw%d_%d" % (o, u), align_bytes=64)
+                entries = offs_list[:, u * S // 32 : (u + 1) * S // 32]
+                nc.vector.tensor_copy(words[:], xw_win[o][:].bitcast(U32).indirect(entries))
+                xw[o].extend(words[:, P * b : P * (b + 1)] for b in range(BLOCKS // 2))
 
-        def gather_x(o, u, words):
-            entries = offs_list[:, u * S // 32 : (u + 1) * S // 32]
-            nc.vector.tensor_copy(words[:], xw_win[o][:].bitcast(U32).indirect(entries))
-            xw[o].extend(words[:, P * b : P * (b + 1)] for b in range(BLOCKS // 2))
-
-        gather_x(0, 0, keep.tile([P, S // 2], U32, name="xw0_0", align_bytes=64))
-        w_mx = [quantize_w(0)]
-        gather_x(0, 1, after_cast.tile([P, S // 2], U32, name="xw0_1", offset=6 * S, align_bytes=64))
-        w_mx.append(quantize_w(1))
-        for u in range(2):
-            gather_x(1, u, after_cast.tile([P, S // 2], U32, name="xw1_%d" % u, offset=2 * S * u, align_bytes=64))
-
-        hv_col = after_cast.tile([P, 2, D], F32, name="hv_col", offset=4 * S)
+        hv_col = keep.tile([P, 2, D], F32, name="hv_col", tag="w_raw1")
         neg_half = hv_col[:, 0, :]
         val_col = hv_col[:, 1, :]
         for a in range(D // PACK):
@@ -146,12 +136,15 @@ def tile_picked_ynw_avg_p_kernel(
             nc.scalar.mul(neg_half[:, PACK * a : PACK * (a + 1)], hv_ps[:, :, HALF_ROW], -1.0)
             nc.scalar.copy(val_col[:, PACK * a : PACK * (a + 1)], hv_ps[:, :, VAL_ROW])
 
-        ew_ex = keep.tile([P, U], U32, name="ew_ex")
-        nc.vector.tensor_copy(ew_ex[:], ew_win[:].bitcast(U32).indirect(ex_list[:]))
+        ew_cuts = [(0, FIRST_GROUPS), (FIRST_GROUPS, V)]
+        ew_ex = [keep.tile([P, D * (end - first)], U32, name="ew_ex%d" % first) for first, end in ew_cuts]
+        for u, (first, end) in enumerate(ew_cuts):
+            entries = ex_list[:, first * D // 16 : end * D // 16]
+            nc.vector.tensor_copy(ew_ex[u][:], ew_win[:].bitcast(U32).indirect(entries))
 
 
         h_bf = late.tile([P, S, PACK], BF16, name="h_bf", offset=0, align_bytes=64)
-        h_codes = keep.tile([P, S], U32, name="h_codes", align_bytes=64)
+        h_codes = e_side.tile([P, S], U32, name="h_codes", offset=0, align_bytes=64)
         h_scales = keep.tile([P, S], U8, name="h_scales", align_bytes=64)
         h_ps = [banks.tile([P, PACK, P], F32, name="h_ps%d" % b, tag="bank%d" % b) for b in range(BLOCKS)]
         for o in range(PASSES):
@@ -174,24 +167,26 @@ def tile_picked_ynw_avg_p_kernel(
         e_codes = []
         e_bytes = []
 
-        def deal(first, count, codes, scale_bytes):
-            members = slice(first, first + count)
+        def deal_bytes(first, count, scale_bytes):
             nc.vector.tensor_copy(
                 scale_bytes[:].rearrange("p (c v) -> p v c", c=count),
-                es_ex[:].rearrange("p (v d) -> p v d", d=D)[:, :, members],
+                es_planes[:].rearrange("p (v d) -> p v d", d=D)[:, :, first : first + count],
             )
-            nc.vector.tensor_copy(
-                codes[:].rearrange("p (c vq vl) -> p vq c vl", c=count, vl=4),
-                ew_ex[:].rearrange("p (vq vl d) -> p vq d vl", d=D, vl=4)[:, :, members, :],
-            )
-            e_codes.extend(codes[:, V * c : V * (c + 1)] for c in range(count))
             e_bytes.extend(scale_bytes[E_PLANE:P, V * c : V * (c + 1)] for c in range(count))
 
+        def deal_words(first, count, codes, u):
+            nc.vector.tensor_copy(
+                codes[:].rearrange("p (c vq vl) -> p vq c vl", c=count, vl=4)[:, ew_cuts[u][0] // 4 : ew_cuts[u][1] // 4],
+                ew_ex[u][:].rearrange("p (vq vl d) -> p vq d vl", d=D, vl=4)[:, :, first : first + count, :],
+            )
+
         codes01 = keep.tile([P, 2 * V], U32, name="codes01", align_bytes=64)
-        bytes01 = keep.tile([P, 2 * V], U8, name="bytes01", tag="w_bf1", align_bytes=64)
-        deal(0, 2, codes01, bytes01)
+        bytes01 = keep.tile([P, 2 * V], U8, name="bytes01", align_bytes=64)
+        deal_bytes(0, 2, bytes01)
+        e_codes.extend(codes01[:, V * c : V * (c + 1)] for c in range(2))
         halves = [slice(0, S // 2), slice(S // 2, S)]
-        for part in halves:
+        for u, part in enumerate(halves):
+            deal_words(0, 2, codes01, u)
             nc.vector.quantize_mx(
                 h_codes[:, part].bitcast(FP8X4), h_scales[:, part], h_bf[:, part, :].rearrange("p n t -> p (n t)")
             )
@@ -199,7 +194,10 @@ def tile_picked_ynw_avg_p_kernel(
             offset = 5 * V * (first - 2)
             codes = late.tile([P, count * V], U32, name="codes%d" % first, offset=offset, align_bytes=64)
             scale_bytes = late.tile([P, count * V], U8, name="bytes%d" % first, offset=offset + 4 * count * V, align_bytes=64)
-            deal(first, count, codes, scale_bytes)
+            deal_bytes(first, count, scale_bytes)
+            for u in range(2):
+                deal_words(first, count, codes, u)
+            e_codes.extend(codes[:, V * c : V * (c + 1)] for c in range(count))
 
         ee = [keep.tile([P, S], F32, name="ee%d" % d) for d in range(D)]
 

@@ -201,7 +201,7 @@ def tile_picked_ynw_avg_p_kernel(
 
         ee = [keep.tile([P, S], F32, name="ee%d" % d) for d in range(D)]
 
-        def weigh(d, y_ps, part):
+        def multiply(d, y_ps, part):
             nc.tensor.matmul_mx(
                 y_ps,
                 lhsT=e_codes[d].bitcast(FP8X4),
@@ -211,53 +211,65 @@ def tile_picked_ynw_avg_p_kernel(
                 start=True,
                 stop=True,
             )
+
+        def weigh(d, y_ps, part):
             nc.scalar.activation(ee[d][:, part], y_ps, EXP, bias=neg_half[:, d : d + 1], scale=0.5)
 
         y_first = sums.tile([P, S // 2], F32, name="y_first", tag="sum")
+        multiply(0, y_first[:], halves[0])
         weigh(0, y_first[:], halves[0])
+        y = []
         for d in range(D):
-            y_ps = banks.tile([P, S], F32, name="y_ps", tag="bank%d" % (d % BLOCKS))
+            y.append(banks.tile([P, S], F32, name="y_ps", tag="bank%d" % (d % BLOCKS)))
             part = halves[1] if d == 0 else slice(0, S)
-            weigh(d, y_ps[:, part], part)
-
-        table_warm = keep.tile([P, 1], F32, name="table_warm")
-        nc.scalar.activation(table_warm[:], ee[D - 2][:, 0:1], RSQRT)
+            multiply(d, y[d][:, part], part)
+            if d < D - 2:
+                weigh(d, y[d][:, part], part)
+        for part in halves:
+            for d in (D - 2, D - 1):
+                weigh(d, y[d][:, part], part)
 
         acc = [keep.tile([P, S], F32, name="acc%d" % i) for i in range(2)]
         for d in range(2):
             nc.vector.tensor_scalar(acc[d][:], ee[d][:], val_col[:, d : d + 1], None, MULT)
         first_two = keep.tile([P, S], F32, name="first_two")
         nc.vector.tensor_tensor(first_two[:], ee[0][:], ee[1][:], ADD)
-        for d in range(2, D - 1):
+        for d in range(2, D - 2):
             nc.vector.scalar_tensor_tensor(acc[d % 2][:], ee[d][:], val_col[:, d : d + 1], acc[d % 2][:], MULT, ADD)
         for part in halves:
-            nc.vector.scalar_tensor_tensor(
-                acc[1][:, part], ee[D - 1][:, part], val_col[:, D - 1 : D], acc[1][:, part], MULT, ADD
-            )
+            for d in (D - 2, D - 1):
+                nc.vector.scalar_tensor_tensor(
+                    acc[d % 2][:, part], ee[d][:, part], val_col[:, d : d + 1], acc[d % 2][:, part], MULT, ADD
+                )
 
         def add_turned(dst, term, b, start, stop):
             nc.tensor.matmul(dst, term[:, P * b : P * (b + 1)], ident[:], is_transpose=True, start=start, stop=stop)
 
-        den_v = sums.tile([P, V], F32, name="den_v", tag="sum")
-        den_s = sums.tile([P, BLOCKS - 1, V], F32, name="den_s", tag="sum")
+        den = [sums.tile([P, n, V], F32, name="den%d" % g, tag="sum") for g, n in enumerate((1, 1, 2))]
         num = [banks.tile([P, 2, V], F32, name="num%d" % g, tag="bank%d" % (BLOCKS - 1 - g)) for g in range(2)]
         den_terms = [first_two] + ee[2:]
-        for i, term in enumerate(den_terms):
-            final = i == len(den_terms) - 1
-            add_turned(den_v[:], term, 0, i == 0, final)
-            for b in range(1, BLOCKS):
-                add_turned(den_s[:, b - 1, :], term, b, i == 0 and b == 1, final and b == BLOCKS - 1)
+
+        def add_to_den(i, blocks):
+            for b in blocks:
+                start, stop = i == 0 and b != 3, i == len(den_terms) - 1 and b != 2
+                add_turned(den[min(b, 2)][:, b // 3, :], den_terms[i], b, start, stop)
+
+        for i in range(len(den_terms) - 2):
+            add_to_den(i, range(BLOCKS))
+        for blocks in ((1, 0), (2, 3)):
+            for i in (len(den_terms) - 2, len(den_terms) - 1):
+                add_to_den(i, blocks)
         for g in range(2):
             for i in range(2):
                 for b in range(2):
                     add_turned(num[g][:, b, :], acc[i], 2 * g + b, i == 0 and b == 0, i == 1 and b == 1)
 
         out_rows = out.rearrange("(b p) v -> p b v", p=P)
-        rec_v = keep.tile([P, V], F32, name="rec_v")
-        nc.vector.reciprocal(rec_v[:], den_v[:])
+        rec_v = keep.tile([P, 1, V], F32, name="rec_v")
+        nc.vector.reciprocal(rec_v[:], den[0][:])
         root = keep.tile([P, BLOCKS - 1, V], F32, name="root")
-        nc.scalar.activation(root[:, 0, :], den_s[:, 0, :], RSQRT)
-        nc.scalar.activation(root[:, 1:3, :], den_s[:, 1:3, :], RSQRT)
+        nc.scalar.activation(root[:, 0:1, :], den[1][:], RSQRT)
+        nc.scalar.activation(root[:, 1:3, :], den[2][:], RSQRT)
         rec_s = keep.tile([P, 2, V], F32, name="rec_s")
         nc.scalar.activation(rec_s[:], root[:, 1:3, :], SQUARE)
 
@@ -268,6 +280,6 @@ def tile_picked_ynw_avg_p_kernel(
 
         once = keep.tile([P, 1, V], F32, name="once")
         nc.vector.tensor_tensor(once[:], num[0][:, 1:2, :], root[:, 0:1, :], MULT)
-        finish(0, 1, num[0][:, 0:1, :], rec_v[:].unsqueeze(1))
+        finish(0, 1, num[0][:, 0:1, :], rec_v[:])
         finish(1, 2, once[:], root[:, 0:1, :])
         finish(2, 4, num[1][:], rec_s[:])

@@ -37,6 +37,7 @@ HALF_ROW = P - 2
 VAL_ROW = P - 1
 E_PLANE = 8
 FIRST_GROUPS = 96
+SCALAR_CLEARS = 1536
 FLOPS = 2 * K * H * S + 2 * H * S * U
 
 
@@ -66,7 +67,7 @@ def tile_picked_ynw_avg_p_kernel(
         nc.vector.memset(es_win[0:16, :].bitcast(I32), 0)
         nc.gpsimd.memset(es_win[32:64, :].bitcast(I32), 0)
         nc.gpsimd.memset(es_win[64:P, :].bitcast(I32), 0)
-        nc.scalar.copy(hv_win[0:HALF_ROW, :], zero[0:HALF_ROW, :].to_broadcast([HALF_ROW, W]))
+        nc.gpsimd.memset(hv_win[0:HALF_ROW, SCALAR_CLEARS:W], 0.0)
         nc.vector.memset(es_planes[:].bitcast(I32), 0)
 
         def load_w(o):
@@ -76,7 +77,8 @@ def tile_picked_ynw_avg_p_kernel(
         nc.sync.dma_start(ex_list[:], ex)
         nc.sync.dma_start(es_win[16:32, :].bitcast(I32), e_scales[0].bitcast(I32))
         nc.scalar.dma_start(hv_win[HALF_ROW : HALF_ROW + 1, :], half[0:1, :])
-        nc.sync.dma_start(hv_win[VAL_ROW : VAL_ROW + 1, :], val[0:1, :])
+        nc.scalar.dma_start(hv_win[VAL_ROW : VAL_ROW + 1, :], val[0:1, :])
+        nc.scalar.copy(hv_win[0:HALF_ROW, 0:SCALAR_CLEARS], zero[0:HALF_ROW, :].to_broadcast([HALF_ROW, SCALAR_CLEARS]))
         load_w(0)
         for q in range(QUADRANTS):
             nc.sync.dma_start(

@@ -12,6 +12,7 @@ U8 = mybir.dt.uint8
 FP8X4 = mybir.dt.float8_e4m3fn_x4
 MULT = mybir.AluOpType.mult
 ADD = mybir.AluOpType.add
+COPY = mybir.ActivationFunctionType.Copy
 EXP = mybir.ActivationFunctionType.Exp
 RSQRT = mybir.ActivationFunctionType.Abs_reciprocal_sqrt
 SQUARE = mybir.ActivationFunctionType.Square
@@ -37,7 +38,8 @@ HALF_ROW = P - 2
 VAL_ROW = P - 1
 E_PLANE = 8
 FIRST_GROUPS = 96
-SCALAR_CLEARS = 1536
+CLEAR_CUTS = (512, 1536)
+VECTOR_CASTS = (48, 48)
 FLOPS = 2 * K * H * S + 2 * H * S * U
 
 
@@ -49,14 +51,15 @@ def tile_picked_ynw_avg_p_kernel(
         keep = ctx.enter_context(tc.tile_pool(name="keep", bufs=1))
         late = ctx.enter_context(tc.tile_pool(name="late", bufs=1))
         e_side = ctx.enter_context(tc.tile_pool(name="e_side", bufs=1))
+        hv_side = ctx.enter_context(tc.tile_pool(name="hv_side", bufs=1))
         banks = ctx.enter_context(tc.psum_pool(name="banks", bufs=1))
         sums = ctx.enter_context(tc.psum_pool(name="sums", bufs=BLOCKS))
 
         ex_list = keep.tile([P, U // 16], U16, name="ex_list")
         offs_list = keep.tile([P, S // 16], U16, name="offs_list")
-        hv_win = keep.tile([P, W], F32, name="hv_win")
+        hv_win = hv_side.tile([P, W], F32, name="hv_win", offset=0, align_bytes=64)
         es_win = e_side.tile([P, W], U8, name="es_win", offset=0, align_bytes=64)
-        es_planes = keep.tile([P, U], U8, name="es_planes")
+        es_planes = keep.tile([P, U], U8, name="es_planes", align_bytes=64)
         xs_win = keep.tile([P, T], U8, name="xs_win", align_bytes=64)
         w_raw = [keep.tile([P, PACK, H], F32, name="w_raw%d" % o) for o in range(PASSES)]
         xw_win = [keep.tile([P, T], I32, name="xw_win%d" % o, align_bytes=64) for o in range(PASSES)]
@@ -67,7 +70,8 @@ def tile_picked_ynw_avg_p_kernel(
         nc.vector.memset(es_win[0:16, :].bitcast(I32), 0)
         nc.gpsimd.memset(es_win[32:64, :].bitcast(I32), 0)
         nc.gpsimd.memset(es_win[64:P, :].bitcast(I32), 0)
-        nc.gpsimd.memset(hv_win[0:HALF_ROW, SCALAR_CLEARS:W], 0.0)
+        nc.vector.memset(hv_win[0:HALF_ROW, CLEAR_CUTS[0] : CLEAR_CUTS[1]], 0.0)
+        nc.gpsimd.memset(hv_win[0:HALF_ROW, CLEAR_CUTS[1] : W], 0.0)
         nc.vector.memset(es_planes[:].bitcast(I32), 0)
 
         def load_w(o):
@@ -78,7 +82,7 @@ def tile_picked_ynw_avg_p_kernel(
         nc.sync.dma_start(es_win[16:32, :].bitcast(I32), e_scales[0].bitcast(I32))
         nc.scalar.dma_start(hv_win[HALF_ROW : HALF_ROW + 1, :], half[0:1, :])
         nc.scalar.dma_start(hv_win[VAL_ROW : VAL_ROW + 1, :], val[0:1, :])
-        nc.scalar.copy(hv_win[0:HALF_ROW, 0:SCALAR_CLEARS], zero[0:HALF_ROW, :].to_broadcast([HALF_ROW, SCALAR_CLEARS]))
+        nc.scalar.copy(hv_win[0:HALF_ROW, 0 : CLEAR_CUTS[0]], zero[0:HALF_ROW, :].to_broadcast([HALF_ROW, CLEAR_CUTS[0]]))
         load_w(0)
         for q in range(QUADRANTS):
             nc.sync.dma_start(
@@ -95,22 +99,28 @@ def tile_picked_ynw_avg_p_kernel(
 
         es_ex = keep.tile([P, U], U8, name="es_ex")
         nc.vector.tensor_copy(es_ex[:], es_win[:].indirect(ex_list[:]))
+        es_dealt = keep.tile([P, U], U8, name="es_dealt")
+        nc.vector.tensor_copy(
+            es_dealt[:].rearrange("p (a c v) -> p a v c", a=2, c=4), es_ex[:].rearrange("p (v a c) -> p a v c", a=2, c=4)
+        )
+        hv_ex = keep.tile([P, U], F32, name="hv_ex")
+        nc.scalar.activation(hv_ex[:], hv_win[:].indirect(ex_list[:]), COPY)
+        ew_win = e_side.tile([P, W], I32, name="ew_win", offset=0, align_bytes=64)
+        nc.sync.dma_start(ew_win[:], e_words[0].rearrange("p n j -> p (n j)").bitcast(I32))
         for q in range(QUADRANTS):
             first = QUADRANT * q + E_PLANE
             nc.sync.dma_start(
-                es_planes[first : first + 4, :].bitcast(I32), es_ex[16 + 4 * q : 20 + 4 * q, :].bitcast(I32)
+                es_planes[first : first + 4, :].bitcast(I32), es_dealt[16 + 4 * q : 20 + 4 * q, :].bitcast(I32)
             )
-        hv_ex = keep.tile([P, U], F32, name="hv_ex")
-        nc.vector.tensor_copy(hv_ex[:], hv_win[:].indirect(ex_list[:]))
-        ew_win = e_side.tile([P, W], I32, name="ew_win", offset=0, align_bytes=64)
-        nc.sync.dma_start(ew_win[:], e_words[0].rearrange("p n j -> p (n j)").bitcast(I32))
 
         def quantize_w(o):
-            w_bf = keep.tile([P, PACK * H], BF16, name="w_bf%d" % o, align_bytes=64)
-            nc.scalar.copy(
-                w_bf[:].rearrange("p (t m j) -> p m j t", t=PACK, j=PACK),
-                w_raw[o][:].rearrange("p j (m t) -> p m j t", t=PACK),
-            )
+            w_bf = hv_side.tile([P, PACK * H], BF16, name="w_bf%d" % o, offset=2 * PACK * H * o, align_bytes=64)
+            rounded = w_bf[:].rearrange("p (t m j) -> p m j t", t=PACK, j=PACK)
+            raw = w_raw[o][:].rearrange("p j (m t) -> p m j t", t=PACK)
+            cut = VECTOR_CASTS[o]
+            if cut:
+                nc.vector.tensor_copy(rounded[:, 0:cut], raw[:, 0:cut])
+            nc.scalar.copy(rounded[:, cut:P], raw[:, cut:P])
             codes = keep.tile([P, H], U32, name="w_codes%d" % o, align_bytes=64)
             scales = keep.tile([P, H], U8, name="w_scales%d" % o, align_bytes=64)
             nc.vector.quantize_mx(codes[:].bitcast(FP8X4), scales[:], w_bf[:])
@@ -167,14 +177,7 @@ def tile_picked_ynw_avg_p_kernel(
                     nc.scalar.copy(h_bf[:, queries, :], h_ps[b][:].rearrange("p t n -> p n t"))
 
         e_codes = []
-        e_bytes = []
-
-        def deal_bytes(first, count, scale_bytes):
-            nc.vector.tensor_copy(
-                scale_bytes[:].rearrange("p (c v) -> p v c", c=count),
-                es_planes[:].rearrange("p (v d) -> p v d", d=D)[:, :, first : first + count],
-            )
-            e_bytes.extend(scale_bytes[E_PLANE:P, V * c : V * (c + 1)] for c in range(count))
+        e_bytes = [es_planes[E_PLANE:P, V * d : V * (d + 1)] for d in range(D)]
 
         def deal_words(first, count, codes, u):
             nc.vector.tensor_copy(
@@ -183,8 +186,6 @@ def tile_picked_ynw_avg_p_kernel(
             )
 
         codes01 = keep.tile([P, 2 * V], U32, name="codes01", align_bytes=64)
-        bytes01 = keep.tile([P, 2 * V], U8, name="bytes01", align_bytes=64)
-        deal_bytes(0, 2, bytes01)
         e_codes.extend(codes01[:, V * c : V * (c + 1)] for c in range(2))
         halves = [slice(0, S // 2), slice(S // 2, S)]
         for u, part in enumerate(halves):
@@ -193,10 +194,8 @@ def tile_picked_ynw_avg_p_kernel(
                 h_codes[:, part].bitcast(FP8X4), h_scales[:, part], h_bf[:, part, :].rearrange("p n t -> p (n t)")
             )
         for first, count in ((2, 2), (4, 4)):
-            offset = 5 * V * (first - 2)
+            offset = 4 * V * (first - 2)
             codes = late.tile([P, count * V], U32, name="codes%d" % first, offset=offset, align_bytes=64)
-            scale_bytes = late.tile([P, count * V], U8, name="bytes%d" % first, offset=offset + 4 * count * V, align_bytes=64)
-            deal_bytes(first, count, scale_bytes)
             for u in range(2):
                 deal_words(first, count, codes, u)
             e_codes.extend(codes[:, V * c : V * (c + 1)] for c in range(count))

@@ -38,8 +38,8 @@ HALF_ROW = P - 2
 VAL_ROW = P - 1
 E_PLANE = 8
 FIRST_GROUPS = 96
-CLEAR_CUTS = (512, 1536)
-VECTOR_CASTS = (48, 48)
+SCALAR_CLEARS = 768
+E_ROWS = 48
 FLOPS = 2 * K * H * S + 2 * H * S * U
 
 
@@ -52,6 +52,7 @@ def tile_picked_ynw_avg_p_kernel(
         late = ctx.enter_context(tc.tile_pool(name="late", bufs=1))
         e_side = ctx.enter_context(tc.tile_pool(name="e_side", bufs=1))
         hv_side = ctx.enter_context(tc.tile_pool(name="hv_side", bufs=1))
+        x_side = ctx.enter_context(tc.tile_pool(name="x_side", bufs=1))
         banks = ctx.enter_context(tc.psum_pool(name="banks", bufs=1))
         sums = ctx.enter_context(tc.psum_pool(name="sums", bufs=BLOCKS))
 
@@ -62,37 +63,39 @@ def tile_picked_ynw_avg_p_kernel(
         es_planes = keep.tile([P, U], U8, name="es_planes", align_bytes=64)
         xs_win = keep.tile([P, T], U8, name="xs_win", align_bytes=64)
         w_raw = [keep.tile([P, PACK, H], F32, name="w_raw%d" % o) for o in range(PASSES)]
-        xw_win = [keep.tile([P, T], I32, name="xw_win%d" % o, align_bytes=64) for o in range(PASSES)]
+        xw_win = [x_side.tile([P, T], I32, name="xw_win%d" % o, offset=4 * T * o, align_bytes=64) for o in range(PASSES)]
 
-        nc.vector.memset(xs_win[:].bitcast(I32), 0)
+        nc.gpsimd.memset(xs_win[:].bitcast(I32), 0)
         zero = keep.tile([P, 1], F32, name="zero")
-        nc.gpsimd.memset(zero[:], 0.0)
-        nc.vector.memset(es_win[0:16, :].bitcast(I32), 0)
-        nc.gpsimd.memset(es_win[32:64, :].bitcast(I32), 0)
-        nc.gpsimd.memset(es_win[64:P, :].bitcast(I32), 0)
-        nc.vector.memset(hv_win[0:HALF_ROW, CLEAR_CUTS[0] : CLEAR_CUTS[1]], 0.0)
-        nc.gpsimd.memset(hv_win[0:HALF_ROW, CLEAR_CUTS[1] : W], 0.0)
-        nc.vector.memset(es_planes[:].bitcast(I32), 0)
+        nc.vector.memset(zero[:], 0.0)
+        nc.vector.memset(es_win[0:E_ROWS, :].bitcast(I32), 0)
+        nc.vector.memset(es_win[E_ROWS + 16 : P, :].bitcast(I32), 0)
+        nc.vector.memset(hv_win[0:HALF_ROW, SCALAR_CLEARS:W], 0.0)
+        nc.gpsimd.memset(es_planes[:].bitcast(I32), 0)
 
         def load_w(o):
             rows = w1[o * PASS_ROWS : (o + 1) * PASS_ROWS, :]
             nc.sync.dma_start(w_raw[o][:], rows.rearrange("(p j) c -> p j c", j=PACK))
 
         nc.sync.dma_start(ex_list[:], ex)
-        nc.sync.dma_start(es_win[16:32, :].bitcast(I32), e_scales[0].bitcast(I32))
+        nc.sync.dma_start(es_win[E_ROWS : E_ROWS + 16, :].bitcast(I32), e_scales[0].bitcast(I32))
         nc.scalar.dma_start(hv_win[HALF_ROW : HALF_ROW + 1, :], half[0:1, :])
         nc.scalar.dma_start(hv_win[VAL_ROW : VAL_ROW + 1, :], val[0:1, :])
-        nc.scalar.copy(hv_win[0:HALF_ROW, 0 : CLEAR_CUTS[0]], zero[0:HALF_ROW, :].to_broadcast([HALF_ROW, CLEAR_CUTS[0]]))
+        nc.scalar.copy(hv_win[0:HALF_ROW, 0:SCALAR_CLEARS], zero[0:HALF_ROW, :].to_broadcast([HALF_ROW, SCALAR_CLEARS]))
+        nc.sync.dma_start(offs_list[:], offs)
         load_w(0)
         for q in range(QUADRANTS):
             nc.sync.dma_start(
                 xs_win[QUADRANT * q : QUADRANT * q + 4 * PASSES, :].bitcast(I32),
                 x_scales[:, 4 * q : 4 * q + 4, :].bitcast(I32),
             )
-        nc.sync.dma_start(offs_list[:], offs)
-        load_w(1)
-        for o in range(PASSES):
+
+        def load_x(o):
             nc.sync.dma_start(xw_win[o][:], x_words[o].rearrange("p n j -> p (n j)").bitcast(I32))
+
+        load_x(0)
+        load_w(1)
+        load_x(1)
 
         ident = keep.tile([P, P], F32, name="ident")
         make_identity(nc, ident[:])
@@ -101,7 +104,8 @@ def tile_picked_ynw_avg_p_kernel(
         nc.vector.tensor_copy(es_ex[:], es_win[:].indirect(ex_list[:]))
         es_dealt = keep.tile([P, U], U8, name="es_dealt")
         nc.vector.tensor_copy(
-            es_dealt[:].rearrange("p (a c v) -> p a v c", a=2, c=4), es_ex[:].rearrange("p (v a c) -> p a v c", a=2, c=4)
+            es_dealt[:].rearrange("p (d vq vl) -> p vq d vl", d=D, vl=4),
+            es_ex[:].rearrange("p (vq vl d) -> p vq d vl", d=D, vl=4),
         )
         hv_ex = keep.tile([P, U], F32, name="hv_ex")
         nc.scalar.activation(hv_ex[:], hv_win[:].indirect(ex_list[:]), COPY)
@@ -110,19 +114,16 @@ def tile_picked_ynw_avg_p_kernel(
         for q in range(QUADRANTS):
             first = QUADRANT * q + E_PLANE
             nc.sync.dma_start(
-                es_planes[first : first + 4, :].bitcast(I32), es_dealt[16 + 4 * q : 20 + 4 * q, :].bitcast(I32)
+                es_planes[first : first + 4, :].bitcast(I32), es_dealt[E_ROWS + 4 * q : E_ROWS + 4 * q + 4, :].bitcast(I32)
             )
 
         def quantize_w(o):
             w_bf = hv_side.tile([P, PACK * H], BF16, name="w_bf%d" % o, offset=2 * PACK * H * o, align_bytes=64)
             rounded = w_bf[:].rearrange("p (t m j) -> p m j t", t=PACK, j=PACK)
             raw = w_raw[o][:].rearrange("p j (m t) -> p m j t", t=PACK)
-            cut = VECTOR_CASTS[o]
-            if cut:
-                nc.vector.tensor_copy(rounded[:, 0:cut], raw[:, 0:cut])
-            nc.scalar.copy(rounded[:, cut:P], raw[:, cut:P])
+            nc.scalar.copy(rounded, raw)
             codes = keep.tile([P, H], U32, name="w_codes%d" % o, align_bytes=64)
-            scales = keep.tile([P, H], U8, name="w_scales%d" % o, align_bytes=64)
+            scales = x_side.tile([P, H], U8, name="w_scales%d" % o, offset=4 * T * o, align_bytes=64)
             nc.vector.quantize_mx(codes[:].bitcast(FP8X4), scales[:], w_bf[:])
             return codes, scales
 
@@ -131,12 +132,12 @@ def tile_picked_ynw_avg_p_kernel(
         xw = [[], []]
         w_mx = []
         for o in range(PASSES):
-            w_mx.append(quantize_w(o))
             for u in range(2):
                 words = keep.tile([P, S // 2], U32, name="xw%d_%d" % (o, u), align_bytes=64)
                 entries = offs_list[:, u * S // 32 : (u + 1) * S // 32]
                 nc.vector.tensor_copy(words[:], xw_win[o][:].bitcast(U32).indirect(entries))
                 xw[o].extend(words[:, P * b : P * (b + 1)] for b in range(BLOCKS // 2))
+            w_mx.append(quantize_w(o))
 
         hv_col = keep.tile([P, 2, D], F32, name="hv_col", tag="w_raw1")
         neg_half = hv_col[:, 0, :]

@@ -38,8 +38,10 @@ HALF_ROW = P - 2
 VAL_ROW = P - 1
 E_PLANE = 8
 FIRST_GROUPS = 96
-SCALAR_CLEARS = 768
+SCALAR_CLEARS = 512
 E_ROWS = 48
+VECTOR_HV = 416
+GPSIMD_CLEARS = 512
 FLOPS = 2 * K * H * S + 2 * H * S * U
 
 
@@ -59,9 +61,9 @@ def tile_picked_ynw_avg_p_kernel(
         ex_list = keep.tile([P, U // 16], U16, name="ex_list")
         offs_list = keep.tile([P, S // 16], U16, name="offs_list")
         hv_win = hv_side.tile([P, W], F32, name="hv_win", offset=0, align_bytes=64)
-        es_win = e_side.tile([P, W], U8, name="es_win", offset=0, align_bytes=64)
+        es_win = keep.tile([P, W], U8, name="es_win", align_bytes=64)
         es_planes = keep.tile([P, U], U8, name="es_planes", align_bytes=64)
-        xs_win = keep.tile([P, T], U8, name="xs_win", align_bytes=64)
+        xs_win = x_side.tile([P, T], U8, name="xs_win", offset=8 * T, align_bytes=64)
         w_raw = [keep.tile([P, PACK, H], F32, name="w_raw%d" % o) for o in range(PASSES)]
         xw_win = [x_side.tile([P, T], I32, name="xw_win%d" % o, offset=4 * T * o, align_bytes=64) for o in range(PASSES)]
 
@@ -70,7 +72,8 @@ def tile_picked_ynw_avg_p_kernel(
         nc.vector.memset(zero[:], 0.0)
         nc.vector.memset(es_win[0:E_ROWS, :].bitcast(I32), 0)
         nc.vector.memset(es_win[E_ROWS + 16 : P, :].bitcast(I32), 0)
-        nc.vector.memset(hv_win[0:HALF_ROW, SCALAR_CLEARS:W], 0.0)
+        nc.vector.memset(hv_win[0:HALF_ROW, SCALAR_CLEARS : W - GPSIMD_CLEARS], 0.0)
+        nc.gpsimd.memset(hv_win[0:HALF_ROW, W - GPSIMD_CLEARS : W], 0.0)
         nc.gpsimd.memset(es_planes[:].bitcast(I32), 0)
 
         def load_w(o):
@@ -79,23 +82,19 @@ def tile_picked_ynw_avg_p_kernel(
 
         nc.sync.dma_start(ex_list[:], ex)
         nc.sync.dma_start(es_win[E_ROWS : E_ROWS + 16, :].bitcast(I32), e_scales[0].bitcast(I32))
-        nc.scalar.dma_start(hv_win[HALF_ROW : HALF_ROW + 1, :], half[0:1, :])
+        nc.sync.dma_start(hv_win[HALF_ROW : HALF_ROW + 1, :], half[0:1, :])
         nc.scalar.dma_start(hv_win[VAL_ROW : VAL_ROW + 1, :], val[0:1, :])
         nc.scalar.copy(hv_win[0:HALF_ROW, 0:SCALAR_CLEARS], zero[0:HALF_ROW, :].to_broadcast([HALF_ROW, SCALAR_CLEARS]))
-        nc.sync.dma_start(offs_list[:], offs)
         load_w(0)
         for q in range(QUADRANTS):
             nc.sync.dma_start(
                 xs_win[QUADRANT * q : QUADRANT * q + 4 * PASSES, :].bitcast(I32),
                 x_scales[:, 4 * q : 4 * q + 4, :].bitcast(I32),
             )
-
-        def load_x(o):
-            nc.sync.dma_start(xw_win[o][:], x_words[o].rearrange("p n j -> p (n j)").bitcast(I32))
-
-        load_x(0)
+        nc.sync.dma_start(offs_list[:], offs)
         load_w(1)
-        load_x(1)
+        for o in range(PASSES):
+            nc.sync.dma_start(xw_win[o][:], x_words[o].rearrange("p n j -> p (n j)").bitcast(I32))
 
         ident = keep.tile([P, P], F32, name="ident")
         make_identity(nc, ident[:])
@@ -104,11 +103,11 @@ def tile_picked_ynw_avg_p_kernel(
         nc.vector.tensor_copy(es_ex[:], es_win[:].indirect(ex_list[:]))
         es_dealt = keep.tile([P, U], U8, name="es_dealt")
         nc.vector.tensor_copy(
-            es_dealt[:].rearrange("p (d vq vl) -> p vq d vl", d=D, vl=4),
-            es_ex[:].rearrange("p (vq vl d) -> p vq d vl", d=D, vl=4),
+            es_dealt[:].rearrange("p (a c v) -> p a v c", a=2, c=4), es_ex[:].rearrange("p (v a c) -> p a v c", a=2, c=4)
         )
         hv_ex = keep.tile([P, U], F32, name="hv_ex")
-        nc.scalar.activation(hv_ex[:], hv_win[:].indirect(ex_list[:]), COPY)
+        nc.vector.tensor_copy(hv_ex[:, 0:VECTOR_HV], hv_win[:].indirect(ex_list[:, 0 : VECTOR_HV // 16]))
+        nc.scalar.activation(hv_ex[:, VECTOR_HV:U], hv_win[:].indirect(ex_list[:, VECTOR_HV // 16 : U // 16]), COPY)
         ew_win = e_side.tile([P, W], I32, name="ew_win", offset=0, align_bytes=64)
         nc.sync.dma_start(ew_win[:], e_words[0].rearrange("p n j -> p (n j)").bitcast(I32))
         for q in range(QUADRANTS):
@@ -118,12 +117,12 @@ def tile_picked_ynw_avg_p_kernel(
             )
 
         def quantize_w(o):
-            w_bf = hv_side.tile([P, PACK * H], BF16, name="w_bf%d" % o, offset=2 * PACK * H * o, align_bytes=64)
+            w_bf = keep.tile([P, PACK * H], BF16, name="w_bf%d" % o, align_bytes=64)
             rounded = w_bf[:].rearrange("p (t m j) -> p m j t", t=PACK, j=PACK)
             raw = w_raw[o][:].rearrange("p j (m t) -> p m j t", t=PACK)
             nc.scalar.copy(rounded, raw)
             codes = keep.tile([P, H], U32, name="w_codes%d" % o, align_bytes=64)
-            scales = x_side.tile([P, H], U8, name="w_scales%d" % o, offset=4 * T * o, align_bytes=64)
+            scales = x_side.tile([P, H], U8, name="w_scales%d" % o, offset=(8 + o) * T, align_bytes=64)
             nc.vector.quantize_mx(codes[:].bitcast(FP8X4), scales[:], w_bf[:])
             return codes, scales
 
@@ -132,12 +131,12 @@ def tile_picked_ynw_avg_p_kernel(
         xw = [[], []]
         w_mx = []
         for o in range(PASSES):
+            w_mx.append(quantize_w(o))
             for u in range(2):
                 words = keep.tile([P, S // 2], U32, name="xw%d_%d" % (o, u), align_bytes=64)
                 entries = offs_list[:, u * S // 32 : (u + 1) * S // 32]
                 nc.vector.tensor_copy(words[:], xw_win[o][:].bitcast(U32).indirect(entries))
                 xw[o].extend(words[:, P * b : P * (b + 1)] for b in range(BLOCKS // 2))
-            w_mx.append(quantize_w(o))
 
         hv_col = keep.tile([P, 2, D], F32, name="hv_col", tag="w_raw1")
         neg_half = hv_col[:, 0, :]

@@ -81,9 +81,9 @@ def tile_picked_ynw_avg_p_kernel(
             nc.sync.dma_start(w_raw[o][:], rows.rearrange("(p j) c -> p j c", j=PACK))
 
         nc.sync.dma_start(ex_list[:], ex)
-        nc.sync.dma_start(es_win[E_ROWS : E_ROWS + 16, :].bitcast(I32), e_scales[0].bitcast(I32))
         nc.sync.dma_start(hv_win[HALF_ROW : HALF_ROW + 1, :], half[0:1, :])
         nc.scalar.dma_start(hv_win[VAL_ROW : VAL_ROW + 1, :], val[0:1, :])
+        nc.scalar.dma_start(es_win[E_ROWS : E_ROWS + 16, :].bitcast(I32), e_scales[0].bitcast(I32))
         nc.scalar.copy(hv_win[0:HALF_ROW, 0:SCALAR_CLEARS], zero[0:HALF_ROW, :].to_broadcast([HALF_ROW, SCALAR_CLEARS]))
         load_w(0)
         for q in range(QUADRANTS):

@@ -42,6 +42,7 @@ SCALAR_CLEARS = 512
 E_ROWS = 48
 VECTOR_HV = 416
 GPSIMD_CLEARS = 512
+H_BANKS = (0, 1, 2, 0)
 FLOPS = 2 * K * H * S + 2 * H * S * U
 
 
@@ -155,26 +156,34 @@ def tile_picked_ynw_avg_p_kernel(
             nc.vector.tensor_copy(ew_ex[u][:], ew_win[:].bitcast(U32).indirect(entries))
 
 
-        h_bf = late.tile([P, S, PACK], BF16, name="h_bf", offset=0, align_bytes=64)
+        h_bf = [late.tile([P, S // 2, PACK], BF16, name="h_bf%d" % u, offset=PACK * S * u, align_bytes=64) for u in range(2)]
         h_codes = e_side.tile([P, S], U32, name="h_codes", offset=0, align_bytes=64)
         h_scales = keep.tile([P, S], U8, name="h_scales", align_bytes=64)
-        h_ps = [banks.tile([P, PACK, P], F32, name="h_ps%d" % b, tag="bank%d" % b) for b in range(BLOCKS)]
-        for o in range(PASSES):
+        h_ps = {}
+
+        def project(o, b):
             w_codes, w_scales = w_mx[o]
-            for b in range(BLOCKS):
-                queries = slice(P * b, P * (b + 1))
-                for t in range(PACK):
-                    nc.tensor.matmul_mx(
-                        h_ps[b][:, t, :],
-                        lhsT=w_codes[:, P * t : P * (t + 1)].bitcast(FP8X4),
-                        lhsT_scale=w_scales[:, P * t : P * (t + 1)],
-                        rhs=xw[o][b].bitcast(FP8X4),
-                        rhs_scale=xs[4 * o : P, queries],
-                        start=(o == 0 and t == 0),
-                        stop=(o == PASSES - 1 and t == PACK - 1),
-                    )
-                if o == PASSES - 1:
-                    nc.scalar.copy(h_bf[:, queries, :], h_ps[b][:].rearrange("p t n -> p n t"))
+            queries = slice(P * b, P * (b + 1))
+            if o == 0:
+                h_ps[b] = banks.tile([P, PACK, P], F32, name="h_ps%d" % b, tag="bank%d" % H_BANKS[b])
+            for t in range(PACK):
+                nc.tensor.matmul_mx(
+                    h_ps[b][:, t, :],
+                    lhsT=w_codes[:, P * t : P * (t + 1)].bitcast(FP8X4),
+                    lhsT_scale=w_scales[:, P * t : P * (t + 1)],
+                    rhs=xw[o][b].bitcast(FP8X4),
+                    rhs_scale=xs[4 * o : P, queries],
+                    start=(o == 0 and t == 0),
+                    stop=(o == PASSES - 1 and t == PACK - 1),
+                )
+            if o == PASSES - 1:
+                nc.scalar.copy(h_bf[b // 2][:, P * (b % 2) : P * (b % 2 + 1), :], h_ps[b][:].rearrange("p t n -> p n t"))
+
+        for o in range(PASSES):
+            for b in range(BLOCKS - 1):
+                project(o, b)
+        for o in range(PASSES):
+            project(o, BLOCKS - 1)
 
         e_codes = []
         e_bytes = [es_planes[E_PLANE:P, V * d : V * (d + 1)] for d in range(D)]
@@ -188,17 +197,25 @@ def tile_picked_ynw_avg_p_kernel(
         codes01 = keep.tile([P, 2 * V], U32, name="codes01", align_bytes=64)
         e_codes.extend(codes01[:, V * c : V * (c + 1)] for c in range(2))
         halves = [slice(0, S // 2), slice(S // 2, S)]
-        for u, part in enumerate(halves):
-            deal_words(0, 2, codes01, u)
+
+        def quantize_h(u):
+            part = halves[u]
             nc.vector.quantize_mx(
-                h_codes[:, part].bitcast(FP8X4), h_scales[:, part], h_bf[:, part, :].rearrange("p n t -> p (n t)")
+                h_codes[:, part].bitcast(FP8X4), h_scales[:, part], h_bf[u][:].rearrange("p n t -> p (n t)")
             )
-        for first, count in ((2, 2), (4, 4)):
-            offset = 4 * V * (first - 2)
+
+        def deal_late(first, count, offset):
             codes = late.tile([P, count * V], U32, name="codes%d" % first, offset=offset, align_bytes=64)
             for u in range(2):
                 deal_words(first, count, codes, u)
             e_codes.extend(codes[:, V * c : V * (c + 1)] for c in range(count))
+
+        deal_words(0, 2, codes01, 0)
+        quantize_h(0)
+        deal_words(0, 2, codes01, 1)
+        deal_late(2, 2, 0)
+        quantize_h(1)
+        deal_late(4, 4, PACK * S)
 
         ee = [keep.tile([P, S], F32, name="ee%d" % d) for d in range(D)]
 
@@ -216,13 +233,17 @@ def tile_picked_ynw_avg_p_kernel(
         def weigh(d, y_ps, part):
             nc.scalar.activation(ee[d][:, part], y_ps, EXP, bias=neg_half[:, d : d + 1], scale=0.5)
 
-        y_first = sums.tile([P, S // 2], F32, name="y_first", tag="sum")
-        multiply(0, y_first[:], halves[0])
-        weigh(0, y_first[:], halves[0])
+        y_first = [
+            sums.tile([P, S // 2], F32, name="y_first0", tag="sum"),
+            banks.tile([P, S // 2], F32, name="y_first1", tag="bank3"),
+        ]
+        for d in range(2):
+            multiply(d, y_first[d][:], halves[0])
+            weigh(d, y_first[d][:], halves[0])
         y = []
         for d in range(D):
-            y.append(banks.tile([P, S], F32, name="y_ps", tag="bank%d" % (d % BLOCKS)))
-            part = halves[1] if d == 0 else slice(0, S)
+            y.append(banks.tile([P, S], F32, name="y_ps", tag="bank%d" % (1, 2, 0, 3)[d % BLOCKS]))
+            part = halves[1] if d < 2 else slice(0, S)
             multiply(d, y[d][:, part], part)
             if d < D - 2:
                 weigh(d, y[d][:, part], part)
@@ -247,7 +268,7 @@ def tile_picked_ynw_avg_p_kernel(
             nc.tensor.matmul(dst, term[:, P * b : P * (b + 1)], ident[:], is_transpose=True, start=start, stop=stop)
 
         den = [sums.tile([P, n, V], F32, name="den%d" % g, tag="sum") for g, n in enumerate((1, 1, 2))]
-        num = [banks.tile([P, 2, V], F32, name="num%d" % g, tag="bank%d" % (BLOCKS - 1 - g)) for g in range(2)]
+        num = [banks.tile([P, 2, V], F32, name="num%d" % g, tag="bank%d" % (1 + g)) for g in range(2)]
         den_terms = [first_two] + ee[2:]
 
         def add_to_den(i, blocks):

@@ -43,6 +43,7 @@ E_ROWS = 48
 VECTOR_HV = 416
 GPSIMD_CLEARS = 512
 H_BANKS = (0, 1, 2, 0)
+BANK_RING = (3, 4, 5, 6, 7, 1, 2, 0)
 FLOPS = 2 * K * H * S + 2 * H * S * U
 
 
@@ -57,7 +58,6 @@ def tile_picked_ynw_avg_p_kernel(
         hv_side = ctx.enter_context(tc.tile_pool(name="hv_side", bufs=1))
         x_side = ctx.enter_context(tc.tile_pool(name="x_side", bufs=1))
         banks = ctx.enter_context(tc.psum_pool(name="banks", bufs=1))
-        sums = ctx.enter_context(tc.psum_pool(name="sums", bufs=BLOCKS))
 
         ex_list = keep.tile([P, U // 16], U16, name="ex_list")
         offs_list = keep.tile([P, S // 16], U16, name="offs_list")
@@ -143,7 +143,7 @@ def tile_picked_ynw_avg_p_kernel(
         neg_half = hv_col[:, 0, :]
         val_col = hv_col[:, 1, :]
         for a in range(D // PACK):
-            hv_ps = sums.tile([P, PACK, P], F32, name="hv_ps", tag="sum")
+            hv_ps = banks.tile([P, PACK, P], F32, name="hv_ps", tag="bank%d" % (BLOCKS + a))
             for c in range(PACK):
                 nc.tensor.transpose(hv_ps[:, c, :], hv_ex[:, PACK * a + c : U : D], ident[:])
             nc.scalar.mul(neg_half[:, PACK * a : PACK * (a + 1)], hv_ps[:, :, HALF_ROW], -1.0)
@@ -233,20 +233,19 @@ def tile_picked_ynw_avg_p_kernel(
         def weigh(d, y_ps, part):
             nc.scalar.activation(ee[d][:, part], y_ps, EXP, bias=neg_half[:, d : d + 1], scale=0.5)
 
-        y_first = [
-            sums.tile([P, S // 2], F32, name="y_first0", tag="sum"),
-            banks.tile([P, S // 2], F32, name="y_first1", tag="bank3"),
-        ]
-        for d in range(2):
-            multiply(d, y_first[d][:], halves[0])
-            weigh(d, y_first[d][:], halves[0])
-        y = []
-        for d in range(D):
-            y.append(banks.tile([P, S], F32, name="y_ps", tag="bank%d" % (1, 2, 0, 3)[d % BLOCKS]))
-            part = halves[1] if d < 2 else slice(0, S)
-            multiply(d, y[d][:, part], part)
-            if d < D - 2:
-                weigh(d, y[d][:, part], part)
+        def bank(n, shape, name):
+            return banks.tile(shape, F32, name=name, tag="bank%d" % BANK_RING[n % len(BANK_RING)])
+
+        for u, part in enumerate(halves):
+            for d in range(2):
+                y_half = bank(2 * u + d, [P, S // 2], "y_half")
+                multiply(d, y_half[:], part)
+                weigh(d, y_half[:], part)
+        y = {d: bank(2 + d, [P, S], "y_ps%d" % d) for d in range(2, D)}
+        for d in range(2, D):
+            multiply(d, y[d][:], slice(0, S))
+        for d in range(2, D - 2):
+            weigh(d, y[d][:], slice(0, S))
         for part in halves:
             for d in (D - 2, D - 1):
                 weigh(d, y[d][:, part], part)
@@ -267,8 +266,8 @@ def tile_picked_ynw_avg_p_kernel(
         def add_turned(dst, term, b, start, stop):
             nc.tensor.matmul(dst, term[:, P * b : P * (b + 1)], ident[:], is_transpose=True, start=start, stop=stop)
 
-        den = [sums.tile([P, n, V], F32, name="den%d" % g, tag="sum") for g, n in enumerate((1, 1, 2))]
-        num = [banks.tile([P, 2, V], F32, name="num%d" % g, tag="bank%d" % (1 + g)) for g in range(2)]
+        den = [bank(D + 2 + g, [P, n, V], "den%d" % g) for g, n in enumerate((1, 1, 2))]
+        num = [bank(D + 5 + g, [P, 2, V], "num%d" % g) for g in range(2)]
         den_terms = [first_two] + ee[2:]
 
         def add_to_den(i, blocks):

@@ -251,10 +251,11 @@ def tile_picked_ynw_avg_p_kernel(
                 weigh(d, y[d][:, part], part)
 
         acc = [keep.tile([P, S], F32, name="acc%d" % i) for i in range(2)]
-        for d in range(2):
-            nc.vector.tensor_scalar(acc[d][:], ee[d][:], val_col[:, d : d + 1], None, MULT)
         first_two = keep.tile([P, S], F32, name="first_two")
-        nc.vector.tensor_tensor(first_two[:], ee[0][:], ee[1][:], ADD)
+        for part in halves:
+            for d in range(2):
+                nc.vector.tensor_scalar(acc[d][:, part], ee[d][:, part], val_col[:, d : d + 1], None, MULT)
+            nc.vector.tensor_tensor(first_two[:, part], ee[0][:, part], ee[1][:, part], ADD)
         for d in range(2, D - 2):
             nc.vector.scalar_tensor_tensor(acc[d % 2][:], ee[d][:], val_col[:, d : d + 1], acc[d % 2][:], MULT, ADD)
         for part in halves:
@@ -266,8 +267,8 @@ def tile_picked_ynw_avg_p_kernel(
         def add_turned(dst, term, b, start, stop):
             nc.tensor.matmul(dst, term[:, P * b : P * (b + 1)], ident[:], is_transpose=True, start=start, stop=stop)
 
-        den = [bank(D + 2 + g, [P, n, V], "den%d" % g) for g, n in enumerate((1, 1, 2))]
-        num = [bank(D + 5 + g, [P, 2, V], "num%d" % g) for g in range(2)]
+        den = [bank(4 + g, [P, n, V], "den%d" % g) for g, n in enumerate((1, 1, 2))]
+        num = [bank(2 + g, [P, 2, V], "num%d" % g) for g in range(2)]
         den_terms = [first_two] + ee[2:]
 
         def add_to_den(i, blocks):
@@ -290,9 +291,11 @@ def tile_picked_ynw_avg_p_kernel(
         nc.vector.reciprocal(rec_v[:], den[0][:])
         root = keep.tile([P, BLOCKS - 1, V], F32, name="root")
         nc.scalar.activation(root[:, 0:1, :], den[1][:], RSQRT)
-        nc.scalar.activation(root[:, 1:3, :], den[2][:], RSQRT)
+        for i in range(2):
+            nc.scalar.activation(root[:, 1 + i, :], den[2][:, i, :], RSQRT)
         rec_s = keep.tile([P, 2, V], F32, name="rec_s")
-        nc.scalar.activation(rec_s[:], root[:, 1:3, :], SQUARE)
+        for i in range(2):
+            nc.scalar.activation(rec_s[:, i, :], root[:, 1 + i, :], SQUARE)
 
         def finish(first, end, numerator, factor):
             res = keep.tile([P, end - first, V], F32, name="res%d" % first)
@@ -303,4 +306,5 @@ def tile_picked_ynw_avg_p_kernel(
         nc.vector.tensor_tensor(once[:], num[0][:, 1:2, :], root[:, 0:1, :], MULT)
         finish(0, 1, num[0][:, 0:1, :], rec_v[:])
         finish(1, 2, once[:], root[:, 0:1, :])
-        finish(2, 4, num[1][:], rec_s[:])
+        for i in range(2):
+            finish(2 + i, 3 + i, num[1][:, i : i + 1, :], rec_s[:, i : i + 1, :])

@@ -97,7 +97,7 @@ def tile_picked_ynw_avg_p_kernel(
         for o in range(PASSES):
             nc.sync.dma_start(xw_win[o][:], x_words[o].rearrange("p n j -> p (n j)").bitcast(I32))
 
-        ident = keep.tile([P, P], F32, name="ident")
+        ident = keep.tile([P, P], F32, name="ident", align_bytes=64)
         make_identity(nc, ident[:])
 
         es_ex = keep.tile([P, U], U8, name="es_ex")
@@ -267,8 +267,8 @@ def tile_picked_ynw_avg_p_kernel(
         def add_turned(dst, term, b, start, stop):
             nc.tensor.matmul(dst, term[:, P * b : P * (b + 1)], ident[:], is_transpose=True, start=start, stop=stop)
 
-        den = [bank(4 + g, [P, n, V], "den%d" % g) for g, n in enumerate((1, 1, 2))]
-        num = [bank(2 + g, [P, 2, V], "num%d" % g) for g in range(2)]
+        den = [bank(D + 2 + g, [P, n, V], "den%d" % g) for g, n in enumerate((1, 1, 2))]
+        num = [bank(D + 5 + g, [P, 2, V], "num%d" % g) for g in range(2)]
         den_terms = [first_two] + ee[2:]
 
         def add_to_den(i, blocks):

from contextlib import ExitStack

import concourse.mybir as mybir
from concourse.masks import make_identity

F32 = mybir.dt.float32
BF16 = mybir.dt.bfloat16
I32 = mybir.dt.int32
U32 = mybir.dt.uint32
U16 = mybir.dt.uint16
U8 = mybir.dt.uint8
FP8X4 = mybir.dt.float8_e4m3fn_x4
MULT = mybir.AluOpType.mult
ADD = mybir.AluOpType.add
COPY = mybir.ActivationFunctionType.Copy
EXP = mybir.ActivationFunctionType.Exp
RSQRT = mybir.ActivationFunctionType.Abs_reciprocal_sqrt
SQUARE = mybir.ActivationFunctionType.Square

P = 128
PACK = 4
K = 1024
T = 1024
S = 512
H = 512
W = 2048
U = 1024
D = 8
V = U // D
PASS_ROWS = P * PACK
PASSES = K // PASS_ROWS
QUADRANT = 32
QUADRANTS = P // QUADRANT
BLOCKS = S // P
PARTS = 2
PART_BLOCKS = BLOCKS // PARTS
HALF_ROW = P - 2
VAL_ROW = P - 1
E_PLANE = 8
FIRST_GROUPS = 96
SCALAR_CLEARS = 512
E_ROWS = 48
VECTOR_HV = 416
GPSIMD_CLEARS = 512
H_BANKS = (0, 1, 2, 0)
BANK_RING = (3, 4, 5, 6, 7, 1, 2, 0)
FLOPS = 2 * K * H * S + 2 * H * S * U


def tile_picked_ynw_avg_p_kernel(
    tc, x_words, x_scales, w1, e_words, e_scales, half, val, offs, ex, out
):
    nc = tc.nc
    with ExitStack() as ctx:
        keep = ctx.enter_context(tc.tile_pool(name="keep", bufs=1))
        late = ctx.enter_context(tc.tile_pool(name="late", bufs=1))
        e_side = ctx.enter_context(tc.tile_pool(name="e_side", bufs=1))
        hv_side = ctx.enter_context(tc.tile_pool(name="hv_side", bufs=1))
        x_side = ctx.enter_context(tc.tile_pool(name="x_side", bufs=1))
        banks = ctx.enter_context(tc.psum_pool(name="banks", bufs=1))

        ex_list = keep.tile([P, U // 16], U16, name="ex_list")
        offs_list = keep.tile([P, S // 16], U16, name="offs_list")
        hv_win = hv_side.tile([P, W], F32, name="hv_win", offset=0, align_bytes=64)
        es_win = keep.tile([P, W], U8, name="es_win", align_bytes=64)
        es_planes = keep.tile([P, U], U8, name="es_planes", align_bytes=64)
        xs_win = x_side.tile([P, T], U8, name="xs_win", offset=8 * T, align_bytes=64)
        w_raw = [keep.tile([P, PACK, H], F32, name="w_raw%d" % o) for o in range(PASSES)]
        xw_win = [x_side.tile([P, T], I32, name="xw_win%d" % o, offset=4 * T * o, align_bytes=64) for o in range(PASSES)]

        nc.gpsimd.memset(xs_win[:].bitcast(I32), 0)
        zero = keep.tile([P, 1], F32, name="zero")
        nc.vector.memset(zero[:], 0.0)
        nc.vector.memset(es_win[0:E_ROWS, :].bitcast(I32), 0)
        nc.vector.memset(es_win[E_ROWS + 16 : P, :].bitcast(I32), 0)
        nc.vector.memset(hv_win[0:HALF_ROW, SCALAR_CLEARS : W - GPSIMD_CLEARS], 0.0)
        nc.gpsimd.memset(hv_win[0:HALF_ROW, W - GPSIMD_CLEARS : W], 0.0)
        nc.gpsimd.memset(es_planes[:].bitcast(I32), 0)

        def load_w(o):
            rows = w1[o * PASS_ROWS : (o + 1) * PASS_ROWS, :]
            nc.sync.dma_start(w_raw[o][:], rows.rearrange("(p j) c -> p j c", j=PACK))

        nc.sync.dma_start(ex_list[:], ex)
        nc.sync.dma_start(hv_win[HALF_ROW : HALF_ROW + 1, :], half[0:1, :])
        nc.scalar.dma_start(hv_win[VAL_ROW : VAL_ROW + 1, :], val[0:1, :])
        nc.scalar.dma_start(es_win[E_ROWS : E_ROWS + 16, :].bitcast(I32), e_scales[0].bitcast(I32))
        nc.scalar.copy(hv_win[0:HALF_ROW, 0:SCALAR_CLEARS], zero[0:HALF_ROW, :].to_broadcast([HALF_ROW, SCALAR_CLEARS]))
        load_w(0)
        for q in range(QUADRANTS):
            nc.sync.dma_start(
                xs_win[QUADRANT * q : QUADRANT * q + 4 * PASSES, :].bitcast(I32),
                x_scales[:, 4 * q : 4 * q + 4, :].bitcast(I32),
            )
        nc.sync.dma_start(offs_list[:], offs)
        load_w(1)
        for o in range(PASSES):
            nc.sync.dma_start(xw_win[o][:], x_words[o].rearrange("p n j -> p (n j)").bitcast(I32))

        ident = keep.tile([P, P], F32, name="ident", align_bytes=64)
        make_identity(nc, ident[:])

        es_ex = keep.tile([P, U], U8, name="es_ex")
        nc.vector.tensor_copy(es_ex[:], es_win[:].indirect(ex_list[:]))
        es_dealt = keep.tile([P, U], U8, name="es_dealt")
        nc.vector.tensor_copy(
            es_dealt[:].rearrange("p (a c v) -> p a v c", a=2, c=4), es_ex[:].rearrange("p (v a c) -> p a v c", a=2, c=4)
        )
        hv_ex = keep.tile([P, U], F32, name="hv_ex")
        nc.vector.tensor_copy(hv_ex[:, 0:VECTOR_HV], hv_win[:].indirect(ex_list[:, 0 : VECTOR_HV // 16]))
        nc.scalar.activation(hv_ex[:, VECTOR_HV:U], hv_win[:].indirect(ex_list[:, VECTOR_HV // 16 : U // 16]), COPY)
        ew_win = e_side.tile([P, W], I32, name="ew_win", offset=0, align_bytes=64)
        nc.sync.dma_start(ew_win[:], e_words[0].rearrange("p n j -> p (n j)").bitcast(I32))
        for q in range(QUADRANTS):
            first = QUADRANT * q + E_PLANE
            nc.sync.dma_start(
                es_planes[first : first + 4, :].bitcast(I32), es_dealt[E_ROWS + 4 * q : E_ROWS + 4 * q + 4, :].bitcast(I32)
            )

        def quantize_w(o):
            w_bf = keep.tile([P, PACK * H], BF16, name="w_bf%d" % o, align_bytes=64)
            rounded = w_bf[:].rearrange("p (t m j) -> p m j t", t=PACK, j=PACK)
            raw = w_raw[o][:].rearrange("p j (m t) -> p m j t", t=PACK)
            nc.scalar.copy(rounded, raw)
            codes = keep.tile([P, H], U32, name="w_codes%d" % o, align_bytes=64)
            scales = x_side.tile([P, H], U8, name="w_scales%d" % o, offset=(8 + o) * T, align_bytes=64)
            nc.vector.quantize_mx(codes[:].bitcast(FP8X4), scales[:], w_bf[:])
            return codes, scales

        xs = keep.tile([P, S], U8, name="xs", align_bytes=64)
        nc.vector.tensor_copy(xs[:], xs_win[:].indirect(offs_list[:]))
        xw = [[], []]
        w_mx = []
        for o in range(PASSES):
            w_mx.append(quantize_w(o))
            for u in range(2):
                words = keep.tile([P, S // 2], U32, name="xw%d_%d" % (o, u), align_bytes=64)
                entries = offs_list[:, u * S // 32 : (u + 1) * S // 32]
                nc.vector.tensor_copy(words[:], xw_win[o][:].bitcast(U32).indirect(entries))
                xw[o].extend(words[:, P * b : P * (b + 1)] for b in range(BLOCKS // 2))

        hv_col = keep.tile([P, 2, D], F32, name="hv_col", tag="w_raw1")
        neg_half = hv_col[:, 0, :]
        val_col = hv_col[:, 1, :]
        for a in range(D // PACK):
            hv_ps = banks.tile([P, PACK, P], F32, name="hv_ps", tag="bank%d" % (BLOCKS + a))
            for c in range(PACK):
                nc.tensor.transpose(hv_ps[:, c, :], hv_ex[:, PACK * a + c : U : D], ident[:])
            nc.scalar.mul(neg_half[:, PACK * a : PACK * (a + 1)], hv_ps[:, :, HALF_ROW], -1.0)
            nc.scalar.copy(val_col[:, PACK * a : PACK * (a + 1)], hv_ps[:, :, VAL_ROW])

        ew_cuts = [(0, FIRST_GROUPS), (FIRST_GROUPS, V)]
        ew_ex = [keep.tile([P, D * (end - first)], U32, name="ew_ex%d" % first) for first, end in ew_cuts]
        for u, (first, end) in enumerate(ew_cuts):
            entries = ex_list[:, first * D // 16 : end * D // 16]
            nc.vector.tensor_copy(ew_ex[u][:], ew_win[:].bitcast(U32).indirect(entries))


        h_bf = [late.tile([P, S // 2, PACK], BF16, name="h_bf%d" % u, offset=PACK * S * u, align_bytes=64) for u in range(2)]
        h_codes = e_side.tile([P, S], U32, name="h_codes", offset=0, align_bytes=64)
        h_scales = keep.tile([P, S], U8, name="h_scales", align_bytes=64)
        h_ps = {}

        def project(o, b):
            w_codes, w_scales = w_mx[o]
            queries = slice(P * b, P * (b + 1))
            if o == 0:
                h_ps[b] = banks.tile([P, PACK, P], F32, name="h_ps%d" % b, tag="bank%d" % H_BANKS[b])
            for t in range(PACK):
                nc.tensor.matmul_mx(
                    h_ps[b][:, t, :],
                    lhsT=w_codes[:, P * t : P * (t + 1)].bitcast(FP8X4),
                    lhsT_scale=w_scales[:, P * t : P * (t + 1)],
                    rhs=xw[o][b].bitcast(FP8X4),
                    rhs_scale=xs[4 * o : P, queries],
                    start=(o == 0 and t == 0),
                    stop=(o == PASSES - 1 and t == PACK - 1),
                )
            if o == PASSES - 1:
                nc.scalar.copy(h_bf[b // 2][:, P * (b % 2) : P * (b % 2 + 1), :], h_ps[b][:].rearrange("p t n -> p n t"))

        for o in range(PASSES):
            for b in range(BLOCKS - 1):
                project(o, b)
        for o in range(PASSES):
            project(o, BLOCKS - 1)

        e_codes = []
        e_bytes = [es_planes[E_PLANE:P, V * d : V * (d + 1)] for d in range(D)]

        def deal_words(first, count, codes, u):
            nc.vector.tensor_copy(
                codes[:].rearrange("p (c vq vl) -> p vq c vl", c=count, vl=4)[:, ew_cuts[u][0] // 4 : ew_cuts[u][1] // 4],
                ew_ex[u][:].rearrange("p (vq vl d) -> p vq d vl", d=D, vl=4)[:, :, first : first + count, :],
            )

        codes01 = keep.tile([P, 2 * V], U32, name="codes01", align_bytes=64)
        e_codes.extend(codes01[:, V * c : V * (c + 1)] for c in range(2))
        halves = [slice(0, S // 2), slice(S // 2, S)]

        def quantize_h(u):
            part = halves[u]
            nc.vector.quantize_mx(
                h_codes[:, part].bitcast(FP8X4), h_scales[:, part], h_bf[u][:].rearrange("p n t -> p (n t)")
            )

        def deal_late(first, count, offset):
            codes = late.tile([P, count * V], U32, name="codes%d" % first, offset=offset, align_bytes=64)
            for u in range(2):
                deal_words(first, count, codes, u)
            e_codes.extend(codes[:, V * c : V * (c + 1)] for c in range(count))

        deal_words(0, 2, codes01, 0)
        quantize_h(0)
        deal_words(0, 2, codes01, 1)
        deal_late(2, 2, 0)
        quantize_h(1)
        deal_late(4, 4, PACK * S)

        ee = [keep.tile([P, S], F32, name="ee%d" % d) for d in range(D)]

        def multiply(d, y_ps, part):
            nc.tensor.matmul_mx(
                y_ps,
                lhsT=e_codes[d].bitcast(FP8X4),
                lhsT_scale=e_bytes[d],
                rhs=h_codes[:, part].bitcast(FP8X4),
                rhs_scale=h_scales[:, part],
                start=True,
                stop=True,
            )

        def weigh(d, y_ps, part):
            nc.scalar.activation(ee[d][:, part], y_ps, EXP, bias=neg_half[:, d : d + 1], scale=0.5)

        def bank(n, shape, name):
            return banks.tile(shape, F32, name=name, tag="bank%d" % BANK_RING[n % len(BANK_RING)])

        for u, part in enumerate(halves):
            for d in range(2):
                y_half = bank(2 * u + d, [P, S // 2], "y_half")
                multiply(d, y_half[:], part)
                weigh(d, y_half[:], part)
        y = {d: bank(2 + d, [P, S], "y_ps%d" % d) for d in range(2, D)}
        for d in range(2, D):
            multiply(d, y[d][:], slice(0, S))
        for d in range(2, D - 2):
            weigh(d, y[d][:], slice(0, S))
        for part in halves:
            for d in (D - 2, D - 1):
                weigh(d, y[d][:, part], part)

        acc = [keep.tile([P, S], F32, name="acc%d" % i) for i in range(2)]
        first_two = keep.tile([P, S], F32, name="first_two")
        for part in halves:
            for d in range(2):
                nc.vector.tensor_scalar(acc[d][:, part], ee[d][:, part], val_col[:, d : d + 1], None, MULT)
            nc.vector.tensor_tensor(first_two[:, part], ee[0][:, part], ee[1][:, part], ADD)
        for d in range(2, D - 2):
            nc.vector.scalar_tensor_tensor(acc[d % 2][:], ee[d][:], val_col[:, d : d + 1], acc[d % 2][:], MULT, ADD)
        for part in halves:
            for d in (D - 2, D - 1):
                nc.vector.scalar_tensor_tensor(
                    acc[d % 2][:, part], ee[d][:, part], val_col[:, d : d + 1], acc[d % 2][:, part], MULT, ADD
                )

        def add_turned(dst, term, b, start, stop):
            nc.tensor.matmul(dst, term[:, P * b : P * (b + 1)], ident[:], is_transpose=True, start=start, stop=stop)

        den = [bank(D + 2 + g, [P, n, V], "den%d" % g) for g, n in enumerate((1, 1, 2))]
        num = [bank(D + 5 + g, [P, 2, V], "num%d" % g) for g in range(2)]
        den_terms = [first_two] + ee[2:]

        def add_to_den(i, blocks):
            for b in blocks:
                start, stop = i == 0 and b != 3, i == len(den_terms) - 1 and b != 2
                add_turned(den[min(b, 2)][:, b // 3, :], den_terms[i], b, start, stop)

        for i in range(len(den_terms) - 2):
            add_to_den(i, range(BLOCKS))
        for blocks in ((1, 0), (2, 3)):
            for i in (len(den_terms) - 2, len(den_terms) - 1):
                add_to_den(i, blocks)
        for g in range(2):
            for i in range(2):
                for b in range(2):
                    add_turned(num[g][:, b, :], acc[i], 2 * g + b, i == 0 and b == 0, i == 1 and b == 1)

        out_rows = out.rearrange("(b p) v -> p b v", p=P)
        rec_v = keep.tile([P, 1, V], F32, name="rec_v")
        nc.vector.reciprocal(rec_v[:], den[0][:])
        root = keep.tile([P, BLOCKS - 1, V], F32, name="root")
        nc.scalar.activation(root[:, 0:1, :], den[1][:], RSQRT)
        for i in range(2):
            nc.scalar.activation(root[:, 1 + i, :], den[2][:, i, :], RSQRT)
        rec_s = keep.tile([P, 2, V], F32, name="rec_s")
        for i in range(2):
            nc.scalar.activation(rec_s[:, i, :], root[:, 1 + i, :], SQUARE)

        def finish(first, end, numerator, factor):
            res = keep.tile([P, end - first, V], F32, name="res%d" % first)
            nc.vector.tensor_tensor(res[:], numerator, factor, MULT)
            nc.sync.dma_start(out_rows[:, first:end, :], res[:])

        once = keep.tile([P, 1, V], F32, name="once")
        nc.vector.tensor_tensor(once[:], num[0][:, 1:2, :], root[:, 0:1, :], MULT)
        finish(0, 1, num[0][:, 0:1, :], rec_v[:])
        finish(1, 2, once[:], root[:, 0:1, :])
        for i in range(2):
            finish(2 + i, 3 + i, num[1][:, i : i + 1, :], rec_s[:, i : i + 1, :])
